import numpy as np
import ml_dtypes


def mxq(x, axis, fmt="e4m3"):
    dtype, down = {"e4m3": (ml_dtypes.float8_e4m3fn, 7), "e5m2": (ml_dtypes.float8_e5m2, 14)}[fmt]
    v = np.moveaxis(np.asarray(x, np.float32).astype(ml_dtypes.bfloat16).astype(np.float64), axis, -1)
    blocks = v.reshape(v.shape[:-1] + (-1, 32))
    amax = np.abs(blocks).max(-1, keepdims=True)
    byte = np.maximum(np.where(amax > 0, np.frexp(amax)[1] - 1 + 127, 0) - down, 1)
    scale = np.exp2(byte - 127.0)
    codes = (blocks / scale).astype(np.float32).astype(dtype).astype(np.float64)
    return np.moveaxis((codes * scale).reshape(v.shape), -1, axis)


WIDE = False


def mx_kscale(k):
    if not WIDE:
        return np.ones(k)
    levels = np.array([10, -10, 5, -5, 0])
    if k % 512:
        return np.exp2(np.random.permutation(np.resize(levels, k // 32))).repeat(32)
    a = np.empty((k // 512, 16))
    for p in range(k // 512):
        a[p, :8] = np.random.permutation(np.resize(levels, 8))
        for g in range(8):
            far = levels[np.abs(levels - a[p, g]) >= 10]
            a[p, g + 8] = far[np.random.randint(len(far))]
    return np.exp2(a.ravel()).repeat(32)


def f64(x):
    return np.asarray(x).astype(np.float64)


def striped(idx):
    return np.tile(idx.reshape(-1, 16).T, (8, 1)).astype(np.uint16)


def unstriped(offs):
    return offs[:16].T.reshape(-1).astype(np.int64)


def pack_weight(w):
    k, n = w.shape
    w = f64(np.asarray(w, np.float32).astype(ml_dtypes.bfloat16)).reshape(k // 32, 32, n)
    amax = np.abs(w).max(1)
    byte = np.clip(np.where(amax > 0, np.frexp(amax)[1] - 1 + 127 - 7, 1), 1, 254)
    scaled = (w * np.exp2(127.0 - byte)[:, None, :]).reshape(k, n).astype(np.float32)
    words = np.ascontiguousarray(scaled.reshape(k // 512, 128, 4, n).transpose(0, 1, 3, 2)).astype(ml_dtypes.float8_e4m3fn).view(np.uint8)
    return words, np.ascontiguousarray(byte.astype(np.uint8).reshape(k // 512, 16, n))


def unpack_weight(words, scales):
    g, p, n, _ = words.shape
    vals = np.ascontiguousarray(words).view(ml_dtypes.float8_e4m3fn).astype(np.float64) * np.repeat(np.exp2(scales.astype(np.float64) - 127.0), 8, axis=1)[..., None]
    return vals.transpose(0, 1, 3, 2).reshape(g * 512, n)


def relu(v):
    return np.maximum(v, 0.0)


K, T, S, H, V = 512, 2048, 512, 512, 512


def setup_inputs():
    n = np.random.standard_normal
    s = mx_kscale(K)[:, None]
    u = mx_kscale(H)
    packed_xT = pack_weight(n((K, T)) * s)
    return {
        "x_words": packed_xT[0],
        "x_scales": packed_xT[1],
        "w1": (n((K, H)) / np.sqrt(K) / s).astype(np.float32),
        "unit": (np.random.uniform(0.7, 1.3, (H, 1)) * u[:, None]).astype(np.float32),
        "inv": (np.random.uniform(0.7, 1.3, (H, 1)) / u[:, None] / np.sqrt(H)).astype(np.float32),
        "sim": ((np.random.uniform(size=(S, V)) < 0.2) * 1.0).astype(np.float32),
        "wt": (np.random.uniform(0.5, 2.0, (S, V))).astype(np.float32),
        "offs": striped(np.random.permutation(T)[:S]),
        "other": striped(np.random.permutation(T)[:V]),
    }


def reference(x_words, x_scales, w1, unit, inv, sim, wt, offs, other):
    xq = unpack_weight(x_words, x_scales)[:, unstriped(offs)]
    w1q = mxq(f64(w1), 0, "e4m3")
    ha = f64(unit) * (np.tanh(2.0 * (w1q.T @ xq)))
    x_other = unpack_weight(x_words, x_scales)[:, unstriped(other)]
    hb = f64(inv) * (np.tanh(2.0 * (w1q.T @ x_other)))
    y = mxq(ha, 0, "e4m3").T @ mxq(hb, 0, "e4m3")
    return f64(wt) * (relu(y) + np.log(np.exp(-1.0 * np.abs(y)) + 1.0) - (f64(sim) * y))

@@ -1,0 +1,213 @@
+from contextlib import ExitStack
+
+import concourse.mybir as mybir
+
+K, T, S, H, V = 512, 2048, 512, 512, 512
+FLOPS = 2 * K * H * S + 2 * K * H * V + 2 * H * S * V
+
+F32 = mybir.dt.float32
+BF16 = mybir.dt.bfloat16
+I32 = mybir.dt.int32
+U32 = mybir.dt.uint32
+U16 = mybir.dt.uint16
+U8 = mybir.dt.uint8
+FP8X4 = mybir.dt.float8_e4m3fn_x4
+ACT = mybir.ActivationFunctionType
+ALU = mybir.AluOpType
+
+P = 128
+PACK = 4
+CHUNK = 128
+GATHER = 256
+
+
+def tile_picked_yhnet_loss_p_kernel(
+    tc, x_words, x_scales, w1, unit, inv, sim, wt, offs, other, out
+):
+    nc = tc.nc
+    with ExitStack() as ctx:
+        keep = ctx.enter_context(tc.tile_pool(name="keep", bufs=1))
+        ring = ctx.enter_context(tc.tile_pool(name="ring", bufs=4))
+        psum = ctx.enter_context(tc.psum_pool(name="psum", bufs=1))
+
+        list_b = keep.tile([P, V // 16], U16, name="list_b")
+        list_a = keep.tile([P, S // 16], U16, name="list_a")
+        nc.sync.dma_start(list_b[:], other)
+        nc.sync.dma_start(list_a[:], offs)
+
+        store_scales = keep.tile([P, T], U8, name="store_scales", align_bytes=64)
+        nc.vector.memset(store_scales[:].bitcast(I32), 0)
+
+        w_rows = w1.rearrange("(p j) c -> p j c", j=PACK)
+        w_raw = []
+        for h in range(2):
+            raw = keep.tile([P, PACK, H // 2], F32, name="w_raw%d" % h)
+            nc.sync.dma_start(out=raw[:], in_=w_rows[:, :, h * H // 2 : (h + 1) * H // 2])
+            w_raw.append(raw)
+            if h == 0:
+                for q in range(4):
+                    nc.sync.dma_start(
+                        out=store_scales[32 * q : 32 * q + 4, :].bitcast(I32),
+                        in_=x_scales[0, 4 * q : 4 * q + 4, :].bitcast(I32),
+                    )
+        store_words = keep.tile([P, T], I32, name="store_words", align_bytes=64)
+        nc.sync.dma_start(
+            out=store_words[:],
+            in_=x_words[0].rearrange("p n r -> p (n r)").bitcast(I32),
+        )
+        inv_sb = keep.tile([P, PACK], F32, name="inv_sb")
+        unit_sb = keep.tile([P, PACK], F32, name="unit_sb")
+        nc.sync.dma_start(out=inv_sb[:], in_=inv.rearrange("(p j) o -> p (j o)", j=PACK))
+        nc.sync.dma_start(out=unit_sb[:], in_=unit.rearrange("(p j) o -> p (j o)", j=PACK))
+        sim_sb = keep.tile([P, S // P, V], F32, name="sim_sb")
+        wt_sb = keep.tile([P, S // P, V], F32, name="wt_sb")
+        nc.sync.dma_start(out=sim_sb[:], in_=sim.rearrange("(i p) v -> p i v", p=P))
+        nc.sync.dma_start(out=wt_sb[:], in_=wt.rearrange("(i p) v -> p i v", p=P))
+
+        xb_scales = keep.tile([P, V], U8, name="xb_scales", align_bytes=64)
+        xa_scales = keep.tile([P, S], U8, name="xa_scales", align_bytes=64)
+        nc.vector.tensor_copy(xb_scales[:], store_scales[:].indirect(list_b[:]))
+        nc.vector.tensor_copy(xa_scales[:], store_scales[:].indirect(list_a[:]))
+
+        w_grouped = keep.tile([P, H * PACK], BF16, name="w_grouped", align_bytes=64)
+        w_dst = w_grouped[:].rearrange("p (t m j) -> p m j t", t=PACK, j=PACK)
+        half = P // 2
+        for h in range(2):
+            nc.scalar.activation(
+                out=w_dst[:, h * half : (h + 1) * half],
+                in_=w_raw[h][:].rearrange("p j (m t) -> p m j t", t=PACK),
+                func=ACT.Copy,
+            )
+        w_codes = keep.tile([P, H], U32, name="w_codes", align_bytes=64)
+        w_scales = keep.tile([P, H], U8, name="w_scales", align_bytes=64)
+        nc.vector.quantize_mx(out=w_codes[:].bitcast(FP8X4), scales=w_scales[:], in_=w_grouped[:])
+
+        def gather_words(name, offsets, g):
+            piece = keep.tile([P, GATHER], U32, name="%s%d" % (name, g), align_bytes=64)
+            cols = slice(g * GATHER // 16, (g + 1) * GATHER // 16)
+            nc.vector.tensor_copy(piece[:], store_words[:].bitcast(U32).indirect(offsets[:, cols]))
+            return piece
+
+        xb_words = []
+        xa_words = []
+        for g in range(S // GATHER):
+            xb_words.append(gather_words("xb_words", list_b, g))
+            xa_words.append(gather_words("xa_words", list_a, g))
+
+        def hidden(pieces, scales, c, factor, grouped):
+            piece = pieces[c * CHUNK // GATHER]
+            n0 = c * CHUNK % GATHER
+            pre = psum.tile([P, PACK, CHUNK], F32, name="pre", bufs=3)
+            for t in range(PACK):
+                cols = slice(t * P, (t + 1) * P)
+                nc.tensor.matmul_mx(
+                    out=pre[:, t, :],
+                    lhsT=w_codes[:, cols].bitcast(FP8X4),
+                    lhsT_scale=w_scales[:, cols],
+                    rhs=piece[:, n0 : n0 + CHUNK].bitcast(FP8X4),
+                    rhs_scale=scales[:, c * CHUNK : (c + 1) * CHUNK],
+                    start=True,
+                    stop=True,
+                )
+            steep = ring.tile([P, CHUNK, PACK], F32, name="steep")
+            nc.scalar.activation(
+                out=steep[:], in_=pre[:].rearrange("p t n -> p n t"), func=ACT.Tanh, scale=2.0
+            )
+            nc.vector.tensor_tensor(
+                out=grouped.rearrange("p (n t) -> p n t", t=PACK),
+                in0=steep[:],
+                in1=factor[:].unsqueeze(1).to_broadcast([P, CHUNK, PACK]),
+                op=ALU.mult,
+            )
+
+        hb_grouped = keep.tile([P, V * PACK], BF16, name="hb_grouped", align_bytes=64)
+        hb_codes = keep.tile([P, V], U32, name="hb_codes", align_bytes=64)
+        hb_scales = keep.tile([P, V], U8, name="hb_scales", align_bytes=64)
+        ha_grouped = keep.tile([P, S * PACK], BF16, name="ha_grouped", align_bytes=64)
+        ha_codes = keep.tile([P, S], U32, name="ha_codes", align_bytes=64)
+        ha_scales = keep.tile([P, S], U8, name="ha_scales", align_bytes=64)
+
+        def hidden_b(c):
+            hidden(xb_words, xb_scales, c, inv_sb, hb_grouped[:, c * CHUNK * PACK : (c + 1) * CHUNK * PACK])
+
+        def hidden_a(c):
+            hidden(xa_words, xa_scales, c, unit_sb, ha_grouped[:, c * CHUNK * PACK : (c + 1) * CHUNK * PACK])
+
+        def quantise(grouped, codes, scales, c0, c1):
+            nc.vector.quantize_mx(
+                out=codes[:, c0:c1].bitcast(FP8X4),
+                scales=scales[:, c0:c1],
+                in_=grouped[:, c0 * PACK : c1 * PACK],
+            )
+
+        blocks = []
+
+        def score(c, v0, v1):
+            y = psum.tile([P, v1 - v0], F32, name="y%d" % len(blocks))
+            rows = slice(c * CHUNK, (c + 1) * CHUNK)
+            nc.tensor.matmul_mx(
+                out=y[:],
+                lhsT=ha_codes[:, rows].bitcast(FP8X4),
+                lhsT_scale=ha_scales[:, rows],
+                rhs=hb_codes[:, v0:v1].bitcast(FP8X4),
+                rhs_scale=hb_scales[:, v0:v1],
+                start=True,
+                stop=True,
+            )
+            blocks.append((c, v0, v1, y))
+
+        hidden_b(0)
+        hidden_b(1)
+        hidden_a(0)
+        quantise(hb_grouped, hb_codes, hb_scales, 0, V // 2)
+        quantise(ha_grouped, ha_codes, ha_scales, 0, CHUNK)
+        score(0, 0, V // 2)
+        hidden_b(2)
+        hidden_b(3)
+        hidden_a(1)
+        quantise(hb_grouped, hb_codes, hb_scales, V // 2, V)
+        quantise(ha_grouped, ha_codes, ha_scales, CHUNK, 2 * CHUNK)
+        score(0, V // 2, V)
+        score(1, 0, V)
+        hidden_a(2)
+        hidden_a(3)
+        for c in (2, 3):
+            quantise(ha_grouped, ha_codes, ha_scales, c * CHUNK, (c + 1) * CHUNK)
+            score(c, 0, V)
+
+        decay = keep.tile([P, S // P, V], F32, name="decay")
+        linear = keep.tile([P, S // P, V], F32, name="linear")
+        for c, v0, v1, y in blocks:
+            size = ring.tile([P, v1 - v0], F32, name="size")
+            nc.scalar.activation(out=size[:], in_=y[:], func=ACT.Abs)
+            nc.scalar.activation(out=decay[:, c, v0:v1], in_=size[:], func=ACT.Exp, scale=-1.0)
+        pulls = []
+        for b, (c, v0, v1, y) in enumerate(blocks):
+            pull = keep.tile([P, v1 - v0], F32, name="pull%d" % b)
+            nc.vector.tensor_tensor(out=pull[:], in0=y[:], in1=sim_sb[:, c, v0:v1], op=ALU.mult)
+            pulls.append(pull)
+        for b, (c, v0, v1, y) in enumerate(blocks):
+            nc.vector.scalar_tensor_tensor(
+                out=linear[:, c, v0:v1], in0=y[:], scalar=0.0, in1=pulls[b][:], op0=ALU.max, op1=ALU.subtract
+            )
+
+        last = S // P - 1
+        parts = [(0, 0, V // 2), (0, V // 2, V)]
+        parts = parts + [(c, 0, V) for c in range(1, last)] + [(last, 0, V // 2), (last, V // 2, V)]
+        losses = []
+
+        def finish(b):
+            c, v0, v1 = parts[b]
+            result = keep.tile([P, v1 - v0], F32, name="result%d" % b)
+            nc.vector.tensor_tensor(out=result[:], in0=losses[b][:], in1=wt_sb[:, c, v0:v1], op=ALU.mult)
+            nc.sync.dma_start(out=out[c * P : (c + 1) * P, v0:v1], in_=result[:])
+
+        for b, (c, v0, v1) in enumerate(parts):
+            soft = keep.tile([P, v1 - v0], F32, name="soft%d" % b)
+            nc.scalar.activation(out=soft[:], in_=decay[:, c, v0:v1], func=ACT.Ln, bias=1.0)
+            loss = keep.tile([P, v1 - v0], F32, name="loss%d" % b)
+            nc.vector.tensor_tensor(out=loss[:], in0=soft[:], in1=linear[:, c, v0:v1], op=ALU.add)
+            losses.append(loss)
+            if b > 0:
+                finish(b - 1)
+        finish(len(parts) - 1)

@@ -1,6 +1,7 @@
 from contextlib import ExitStack
 
 import concourse.mybir as mybir
+from concourse.masks import make_identity
 
 K, T, S, H, V = 512, 2048, 512, 512, 512
 FLOPS = 2 * K * H * S + 2 * K * H * V + 2 * H * S * V
@@ -32,8 +33,8 @@ def tile_picked_yhnet_loss_p_kernel(
 
         list_b = keep.tile([P, V // 16], U16, name="list_b")
         list_a = keep.tile([P, S // 16], U16, name="list_a")
-        nc.sync.dma_start(list_b[:], other)
         nc.sync.dma_start(list_a[:], offs)
+        nc.sync.dma_start(list_b[:], other)
 
         store_scales = keep.tile([P, T], U8, name="store_scales", align_bytes=64)
         nc.vector.memset(store_scales[:].bitcast(I32), 0)
@@ -66,8 +67,10 @@ def tile_picked_yhnet_loss_p_kernel(
 
         xb_scales = keep.tile([P, V], U8, name="xb_scales", align_bytes=64)
         xa_scales = keep.tile([P, S], U8, name="xa_scales", align_bytes=64)
-        nc.vector.tensor_copy(xb_scales[:], store_scales[:].indirect(list_b[:]))
         nc.vector.tensor_copy(xa_scales[:], store_scales[:].indirect(list_a[:]))
+        nc.vector.tensor_copy(xb_scales[:], store_scales[:].indirect(list_b[:]))
+        identity = keep.tile([P, P], F32, name="identity")
+        make_identity(nc, identity[:])
 
         w_grouped = keep.tile([P, H * PACK], BF16, name="w_grouped", align_bytes=64)
         w_dst = w_grouped[:].rearrange("p (t m j) -> p m j t", t=PACK, j=PACK)
@@ -91,13 +94,16 @@ def tile_picked_yhnet_loss_p_kernel(
         xb_words = []
         xa_words = []
         for g in range(S // GATHER):
-            xb_words.append(gather_words("xb_words", list_b, g))
             xa_words.append(gather_words("xa_words", list_a, g))
+            xb_words.append(gather_words("xb_words", list_b, g))
+
+        made = []
 
         def hidden(pieces, scales, c, factor, grouped):
             piece = pieces[c * CHUNK // GATHER]
             n0 = c * CHUNK % GATHER
-            pre = psum.tile([P, PACK, CHUNK], F32, name="pre", bufs=3)
+            pre = psum.tile([P, PACK, CHUNK], F32, name="pre", tag="early%d" % (len(made) % 3))
+            made.append(pre)
             for t in range(PACK):
                 cols = slice(t * P, (t + 1) * P)
                 nc.tensor.matmul_mx(
@@ -142,72 +148,95 @@ def tile_picked_yhnet_loss_p_kernel(
 
         blocks = []
 
-        def score(c, v0, v1):
-            y = psum.tile([P, v1 - v0], F32, name="y%d" % len(blocks))
-            rows = slice(c * CHUNK, (c + 1) * CHUNK)
+        def score(k, t0, t1):
+            y = psum.tile([P, t1 - t0], F32, name="y", tag="score%d" % len(blocks))
+            rows = slice(k * CHUNK, (k + 1) * CHUNK)
             nc.tensor.matmul_mx(
                 out=y[:],
-                lhsT=ha_codes[:, rows].bitcast(FP8X4),
-                lhsT_scale=ha_scales[:, rows],
-                rhs=hb_codes[:, v0:v1].bitcast(FP8X4),
-                rhs_scale=hb_scales[:, v0:v1],
+                lhsT=hb_codes[:, rows].bitcast(FP8X4),
+                lhsT_scale=hb_scales[:, rows],
+                rhs=ha_codes[:, t0:t1].bitcast(FP8X4),
+                rhs_scale=ha_scales[:, t0:t1],
                 start=True,
                 stop=True,
             )
-            blocks.append((c, v0, v1, y))
+            blocks.append((k, t0, t1, y))
 
-        hidden_b(0)
-        hidden_b(1)
         hidden_a(0)
-        quantise(hb_grouped, hb_codes, hb_scales, 0, V // 2)
-        quantise(ha_grouped, ha_codes, ha_scales, 0, CHUNK)
-        score(0, 0, V // 2)
-        hidden_b(2)
-        hidden_b(3)
         hidden_a(1)
-        quantise(hb_grouped, hb_codes, hb_scales, V // 2, V)
-        quantise(ha_grouped, ha_codes, ha_scales, CHUNK, 2 * CHUNK)
-        score(0, V // 2, V)
-        score(1, 0, V)
+        hidden_b(0)
+        quantise(ha_grouped, ha_codes, ha_scales, 0, S // 2)
+        quantise(hb_grouped, hb_codes, hb_scales, 0, CHUNK)
+        score(0, 0, S // 2)
         hidden_a(2)
         hidden_a(3)
-        for c in (2, 3):
-            quantise(ha_grouped, ha_codes, ha_scales, c * CHUNK, (c + 1) * CHUNK)
-            score(c, 0, V)
+        quantise(ha_grouped, ha_codes, ha_scales, S // 2, S)
+        score(0, S // 2, S)
+        for k in (1, 2, 3):
+            hidden_b(k)
+            quantise(hb_grouped, hb_codes, hb_scales, k * CHUNK, (k + 1) * CHUNK)
+            score(k, 0, S)
 
-        decay = keep.tile([P, S // P, V], F32, name="decay")
-        linear = keep.tile([P, S // P, V], F32, name="linear")
-        for c, v0, v1, y in blocks:
-            size = ring.tile([P, v1 - v0], F32, name="size")
-            nc.scalar.activation(out=size[:], in_=y[:], func=ACT.Abs)
-            nc.scalar.activation(out=decay[:, c, v0:v1], in_=size[:], func=ACT.Exp, scale=-1.0)
-        pulls = []
-        for b, (c, v0, v1, y) in enumerate(blocks):
-            pull = keep.tile([P, v1 - v0], F32, name="pull%d" % b)
-            nc.vector.tensor_tensor(out=pull[:], in0=y[:], in1=sim_sb[:, c, v0:v1], op=ALU.mult)
-            pulls.append(pull)
-        for b, (c, v0, v1, y) in enumerate(blocks):
-            nc.vector.scalar_tensor_tensor(
-                out=linear[:, c, v0:v1], in0=y[:], scalar=0.0, in1=pulls[b][:], op0=ALU.max, op1=ALU.subtract
+        tiles = V // P
+        half_size = keep.tile([P, tiles, S], F32, name="half_size")
+        decay = keep.tile([P, tiles, S], F32, name="decay")
+        for k, t0, t1, y in blocks:
+            nc.scalar.activation(out=half_size[:, k, t0:t1], in_=y[:], func=ACT.Abs, scale=0.5)
+            nc.scalar.activation(out=decay[:, k, t0:t1], in_=half_size[:, k, t0:t1], func=ACT.Exp, scale=-2.0)
+
+        slope = keep.tile([P, tiles, S], F32, name="slope")
+        slanted = keep.tile([P, tiles, S], F32, name="slanted")
+
+        def make_slope(k):
+            turned = psum.tile([P, S], F32, name="turned", tag="early%d" % (k % 3))
+            for i in range(S // P):
+                nc.tensor.transpose(turned[:, i * P : (i + 1) * P], sim_sb[:, i, k * P : (k + 1) * P], identity[:])
+            nc.vector.tensor_scalar(
+                out=slope[:, k, :], in0=turned[:], scalar1=-1.0, scalar2=0.5, op0=ALU.mult, op1=ALU.add
             )
 
+        def slant(k):
+            for kk, t0, t1, y in blocks:
+                if kk == k:
+                    nc.vector.tensor_tensor(out=slanted[:, k, t0:t1], in0=y[:], in1=slope[:, k, t0:t1], op=ALU.mult)
+
+        make_slope(0)
+        make_slope(1)
+        slant(0)
+        make_slope(2)
+        slant(1)
+        make_slope(3)
+        slant(2)
+        slant(3)
+
         last = S // P - 1
-        parts = [(0, 0, V // 2), (0, V // 2, V)]
-        parts = parts + [(c, 0, V) for c in range(1, last)] + [(last, 0, V // 2), (last, V // 2, V)]
-        losses = []
+        parts = [(i, 0, tiles) for i in range(last)] + [(last, 0, tiles // 2), (last, tiles // 2, tiles)]
+        banks = ("score0", "score1", "early1", "early2", "score2")
+        losses = [
+            psum.tile([P, (k1 - k0) * P], F32, name="loss", tag=tag) for (i, k0, k1), tag in zip(parts, banks)
+        ]
 
-        def finish(b):
-            c, v0, v1 = parts[b]
-            result = keep.tile([P, v1 - v0], F32, name="result%d" % b)
-            nc.vector.tensor_tensor(out=result[:], in0=losses[b][:], in1=wt_sb[:, c, v0:v1], op=ALU.mult)
-            nc.sync.dma_start(out=out[c * P : (c + 1) * P, v0:v1], in_=result[:])
+        def add_turned(loss, column, block, start, stop):
+            nc.tensor.matmul(
+                loss[:, column * P : (column + 1) * P], block, identity[:], start=start, stop=stop, is_transpose=True
+            )
 
-        for b, (c, v0, v1) in enumerate(parts):
-            soft = keep.tile([P, v1 - v0], F32, name="soft%d" % b)
-            nc.scalar.activation(out=soft[:], in_=decay[:, c, v0:v1], func=ACT.Ln, bias=1.0)
-            loss = keep.tile([P, v1 - v0], F32, name="loss%d" % b)
-            nc.vector.tensor_tensor(out=loss[:], in0=soft[:], in1=linear[:, c, v0:v1], op=ALU.add)
-            losses.append(loss)
-            if b > 0:
-                finish(b - 1)
-        finish(len(parts) - 1)
+        def add_term(term, k, opens):
+            for (i, k0, k1), loss in zip(parts, losses):
+                if k0 <= k < k1:
+                    add_turned(loss, k - k0, term[:, k, i * P : (i + 1) * P], opens and k == k0, False)
+
+        add_term(half_size, 0, True)
+        for k in range(1, tiles):
+            add_term(half_size, k, True)
+            add_term(slanted, k - 1, False)
+        add_term(slanted, tiles - 1, False)
+
+        for b, ((i, k0, k1), loss) in enumerate(zip(parts, losses)):
+            soft = keep.tile([P, k1 - k0, P], F32, name="soft%d" % b, tag="soft%d" % (b % last))
+            nc.scalar.activation(out=soft[:], in_=decay[:, k0:k1, i * P : (i + 1) * P], func=ACT.Ln, bias=1.0)
+            for k in range(k0, k1):
+                add_turned(loss, k - k0, soft[:, k - k0, :], False, k == k1 - 1)
+            result = keep.tile([P, (k1 - k0) * P], F32, name="result%d" % b)
+            nc.vector.tensor_tensor(out=result[:], in0=loss[:], in1=wt_sb[:, i, k0 * P : k1 * P], op=ALU.mult)
+            nc.sync.dma_start(out=out[i * P : (i + 1) * P, k0 * P : k1 * P], in_=result[:])

@@ -48,8 +48,8 @@ def tile_picked_yhnet_loss_p_kernel(
             if h == 0:
                 for q in range(4):
                     nc.sync.dma_start(
-                        out=store_scales[32 * q : 32 * q + 4, :].bitcast(I32),
-                        in_=x_scales[0, 4 * q : 4 * q + 4, :].bitcast(I32),
+                        out=store_scales[q:P:32, :].bitcast(I32),
+                        in_=x_scales[0, q:16:4, :].bitcast(I32),
                     )
         store_words = keep.tile([P, T], I32, name="store_words", align_bytes=64)
         nc.sync.dma_start(
@@ -91,18 +91,15 @@ def tile_picked_yhnet_loss_p_kernel(
             nc.vector.tensor_copy(piece[:], store_words[:].bitcast(U32).indirect(offsets[:, cols]))
             return piece
 
-        xb_words = []
-        xa_words = []
-        for g in range(S // GATHER):
-            xa_words.append(gather_words("xa_words", list_a, g))
-            xb_words.append(gather_words("xb_words", list_b, g))
+        xa_words = [gather_words("xa_words", list_a, g) for g in range(S // GATHER)]
+        xb_words = [gather_words("xb_words", list_b, g) for g in range(V // GATHER)]
 
         made = []
 
         def hidden(pieces, scales, c, factor, grouped):
             piece = pieces[c * CHUNK // GATHER]
             n0 = c * CHUNK % GATHER
-            pre = psum.tile([P, PACK, CHUNK], F32, name="pre", tag="early%d" % (len(made) % 3))
+            pre = psum.tile([P, PACK, CHUNK], F32, name="pre", tag="early%d" % (len(made) % 4))
             made.append(pre)
             for t in range(PACK):
                 cols = slice(t * P, (t + 1) * P)
@@ -115,7 +112,7 @@ def tile_picked_yhnet_loss_p_kernel(
                     start=True,
                     stop=True,
                 )
-            steep = ring.tile([P, CHUNK, PACK], F32, name="steep")
+            steep = ring.tile([P, CHUNK, PACK], F32, name="steep", bufs=8)
             nc.scalar.activation(
                 out=steep[:], in_=pre[:].rearrange("p t n -> p n t"), func=ACT.Tanh, scale=2.0
             )
@@ -162,56 +159,58 @@ def tile_picked_yhnet_loss_p_kernel(
             )
             blocks.append((k, t0, t1, y))
 
-        hidden_a(0)
-        hidden_a(1)
+        for c in range(S // CHUNK):
+            hidden_a(c)
         hidden_b(0)
-        quantise(ha_grouped, ha_codes, ha_scales, 0, S // 2)
-        quantise(hb_grouped, hb_codes, hb_scales, 0, CHUNK)
-        score(0, 0, S // 2)
-        hidden_a(2)
-        hidden_a(3)
-        quantise(ha_grouped, ha_codes, ha_scales, S // 2, S)
-        score(0, S // 2, S)
-        for k in (1, 2, 3):
-            hidden_b(k)
+        quantise(ha_grouped, ha_codes, ha_scales, 0, S)
+        for k in range(V // CHUNK):
+            if 0 < k < V // CHUNK - 1:
+                hidden_b(k + 1)
             quantise(hb_grouped, hb_codes, hb_scales, k * CHUNK, (k + 1) * CHUNK)
             score(k, 0, S)
+            if k == 0:
+                hidden_b(1)
 
         tiles = V // P
-        half_size = keep.tile([P, tiles, S], F32, name="half_size")
-        decay = keep.tile([P, tiles, S], F32, name="decay")
+        bent = keep.tile([P, tiles, S], F32, name="bent")
+        size = keep.tile([P, tiles, S], F32, name="size")
         for k, t0, t1, y in blocks:
-            nc.scalar.activation(out=half_size[:, k, t0:t1], in_=y[:], func=ACT.Abs, scale=0.5)
-            nc.scalar.activation(out=decay[:, k, t0:t1], in_=half_size[:, k, t0:t1], func=ACT.Exp, scale=-2.0)
+            nc.scalar.activation(out=bent[:, k, t0:t1], in_=y[:], func=ACT.Tanh, scale=0.5)
+        for k in range(tiles - 1):
+            nc.scalar.activation(out=size[:, k, :], in_=bent[:, k, :], func=ACT.Abs)
 
         slope = keep.tile([P, tiles, S], F32, name="slope")
         slanted = keep.tile([P, tiles, S], F32, name="slanted")
 
         def make_slope(k):
-            turned = psum.tile([P, S], F32, name="turned", tag="early%d" % (k % 3))
+            turned = psum.tile([P, S], F32, name="turned", tag="early%d" % k)
             for i in range(S // P):
                 nc.tensor.transpose(turned[:, i * P : (i + 1) * P], sim_sb[:, i, k * P : (k + 1) * P], identity[:])
-            nc.vector.tensor_scalar(
-                out=slope[:, k, :], in0=turned[:], scalar1=-1.0, scalar2=0.5, op0=ALU.mult, op1=ALU.add
+            nc.vector.scalar_tensor_tensor(
+                out=slope[:, k, :], in0=bent[:, k, :], scalar=0.0, in1=turned[:], op0=ALU.is_gt, op1=ALU.subtract
             )
 
         def slant(k):
             for kk, t0, t1, y in blocks:
                 if kk == k:
-                    nc.vector.tensor_tensor(out=slanted[:, k, t0:t1], in0=y[:], in1=slope[:, k, t0:t1], op=ALU.mult)
+                    nc.vector.scalar_tensor_tensor(
+                        out=slanted[:, k, t0:t1],
+                        in0=y[:],
+                        scalar=-1.0,
+                        in1=slope[:, k, t0:t1],
+                        op0=ALU.mult,
+                        op1=ALU.mult,
+                    )
 
         make_slope(0)
-        make_slope(1)
-        slant(0)
-        make_slope(2)
-        slant(1)
-        make_slope(3)
-        slant(2)
-        slant(3)
+        for k in range(1, tiles):
+            make_slope(k)
+            slant(k - 1)
+        slant(tiles - 1)
 
         last = S // P - 1
         parts = [(i, 0, tiles) for i in range(last)] + [(last, 0, tiles // 2), (last, tiles // 2, tiles)]
-        banks = ("score0", "score1", "early1", "early2", "score2")
+        banks = ("early0", "early1", "score0", "early2", "score1")
         losses = [
             psum.tile([P, (k1 - k0) * P], F32, name="loss", tag=tag) for (i, k0, k1), tag in zip(parts, banks)
         ]
@@ -221,22 +220,21 @@ def tile_picked_yhnet_loss_p_kernel(
                 loss[:, column * P : (column + 1) * P], block, identity[:], start=start, stop=stop, is_transpose=True
             )
 
-        def add_term(term, k, opens):
+        for k in range(tiles):
             for (i, k0, k1), loss in zip(parts, losses):
                 if k0 <= k < k1:
-                    add_turned(loss, k - k0, term[:, k, i * P : (i + 1) * P], opens and k == k0, False)
-
-        add_term(half_size, 0, True)
-        for k in range(1, tiles):
-            add_term(half_size, k, True)
-            add_term(slanted, k - 1, False)
-        add_term(slanted, tiles - 1, False)
+                    add_turned(loss, k - k0, slanted[:, k, i * P : (i + 1) * P], k == k0, False)
 
         for b, ((i, k0, k1), loss) in enumerate(zip(parts, losses)):
+            rows = slice(i * P, (i + 1) * P)
+            if k1 == tiles:
+                nc.scalar.activation(out=size[:, tiles - 1, rows], in_=bent[:, tiles - 1, rows], func=ACT.Abs)
             soft = keep.tile([P, k1 - k0, P], F32, name="soft%d" % b, tag="soft%d" % (b % last))
-            nc.scalar.activation(out=soft[:], in_=decay[:, k0:k1, i * P : (i + 1) * P], func=ACT.Ln, bias=1.0)
+            nc.scalar.activation(out=soft[:], in_=size[:, k0:k1, rows], func=ACT.Ln, scale=0.5, bias=0.5)
             for k in range(k0, k1):
                 add_turned(loss, k - k0, soft[:, k - k0, :], False, k == k1 - 1)
             result = keep.tile([P, (k1 - k0) * P], F32, name="result%d" % b)
-            nc.vector.tensor_tensor(out=result[:], in0=loss[:], in1=wt_sb[:, i, k0 * P : k1 * P], op=ALU.mult)
-            nc.sync.dma_start(out=out[i * P : (i + 1) * P, k0 * P : k1 * P], in_=result[:])
+            nc.vector.scalar_tensor_tensor(
+                out=result[:], in0=loss[:], scalar=-1.0, in1=wt_sb[:, i, k0 * P : k1 * P], op0=ALU.mult, op1=ALU.mult
+            )
+            nc.sync.dma_start(out=out[rows, k0 * P : k1 * P], in_=result[:])

@@ -34,7 +34,6 @@ def tile_picked_yhnet_loss_p_kernel(
         list_b = keep.tile([P, V // 16], U16, name="list_b")
         list_a = keep.tile([P, S // 16], U16, name="list_a")
         nc.sync.dma_start(list_a[:], offs)
-        nc.sync.dma_start(list_b[:], other)
 
         store_scales = keep.tile([P, T], U8, name="store_scales", align_bytes=64)
         nc.vector.memset(store_scales[:].bitcast(I32), 0)
@@ -46,6 +45,7 @@ def tile_picked_yhnet_loss_p_kernel(
             nc.sync.dma_start(out=raw[:], in_=w_rows[:, :, h * H // 2 : (h + 1) * H // 2])
             w_raw.append(raw)
             if h == 0:
+                nc.sync.dma_start(list_b[:], other)
                 for q in range(4):
                     nc.sync.dma_start(
                         out=store_scales[q:P:32, :].bitcast(I32),
@@ -176,7 +176,7 @@ def tile_picked_yhnet_loss_p_kernel(
         size = keep.tile([P, tiles, S], F32, name="size")
         for k, t0, t1, y in blocks:
             nc.scalar.activation(out=bent[:, k, t0:t1], in_=y[:], func=ACT.Tanh, scale=0.5)
-        for k in range(tiles - 1):
+        for k in range(tiles - 2):
             nc.scalar.activation(out=size[:, k, :], in_=bent[:, k, :], func=ACT.Abs)
 
         slope = keep.tile([P, tiles, S], F32, name="slope")
@@ -204,6 +204,10 @@ def tile_picked_yhnet_loss_p_kernel(
 
         make_slope(0)
         for k in range(1, tiles):
+            if k == tiles - 2:
+                nc.vector.scalar_tensor_tensor(
+                    out=size[:, k, :], in0=bent[:, k, :], scalar=-1.0, in1=bent[:, k, :], op0=ALU.mult, op1=ALU.max
+                )
             make_slope(k)
             slant(k - 1)
         slant(tiles - 1)

@@ -1,7 +1,6 @@
 from contextlib import ExitStack
 
 import concourse.mybir as mybir
-from concourse.masks import make_identity
 
 K, T, S, H, V = 512, 2048, 512, 512, 512
 FLOPS = 2 * K * H * S + 2 * K * H * V + 2 * H * S * V
@@ -20,6 +19,7 @@ P = 128
 PACK = 4
 CHUNK = 128
 GATHER = 256
+KNEE = 32.0
 
 
 def tile_picked_yhnet_loss_p_kernel(
@@ -33,7 +33,7 @@ def tile_picked_yhnet_loss_p_kernel(
 
         list_b = keep.tile([P, V // 16], U16, name="list_b")
         list_a = keep.tile([P, S // 16], U16, name="list_a")
-        nc.sync.dma_start(list_a[:], offs)
+        nc.sync.dma_start(list_b[:], other)
 
         store_scales = keep.tile([P, T], U8, name="store_scales", align_bytes=64)
         nc.vector.memset(store_scales[:].bitcast(I32), 0)
@@ -45,7 +45,7 @@ def tile_picked_yhnet_loss_p_kernel(
             nc.sync.dma_start(out=raw[:], in_=w_rows[:, :, h * H // 2 : (h + 1) * H // 2])
             w_raw.append(raw)
             if h == 0:
-                nc.sync.dma_start(list_b[:], other)
+                nc.sync.dma_start(list_a[:], offs)
                 for q in range(4):
                     nc.sync.dma_start(
                         out=store_scales[q:P:32, :].bitcast(I32),
@@ -67,10 +67,8 @@ def tile_picked_yhnet_loss_p_kernel(
 
         xb_scales = keep.tile([P, V], U8, name="xb_scales", align_bytes=64)
         xa_scales = keep.tile([P, S], U8, name="xa_scales", align_bytes=64)
-        nc.vector.tensor_copy(xa_scales[:], store_scales[:].indirect(list_a[:]))
         nc.vector.tensor_copy(xb_scales[:], store_scales[:].indirect(list_b[:]))
-        identity = keep.tile([P, P], F32, name="identity")
-        make_identity(nc, identity[:])
+        nc.vector.tensor_copy(xa_scales[:], store_scales[:].indirect(list_a[:]))
 
         w_grouped = keep.tile([P, H * PACK], BF16, name="w_grouped", align_bytes=64)
         w_dst = w_grouped[:].rearrange("p (t m j) -> p m j t", t=PACK, j=PACK)
@@ -91,15 +89,17 @@ def tile_picked_yhnet_loss_p_kernel(
             nc.vector.tensor_copy(piece[:], store_words[:].bitcast(U32).indirect(offsets[:, cols]))
             return piece
 
-        xa_words = [gather_words("xa_words", list_a, g) for g in range(S // GATHER)]
-        xb_words = [gather_words("xb_words", list_b, g) for g in range(V // GATHER)]
+        xb_words, xa_words = [], []
+        for g in range(S // GATHER):
+            xb_words.append(gather_words("xb_words", list_b, g))
+            xa_words.append(gather_words("xa_words", list_a, g))
 
         made = []
 
         def hidden(pieces, scales, c, factor, grouped):
             piece = pieces[c * CHUNK // GATHER]
             n0 = c * CHUNK % GATHER
-            pre = psum.tile([P, PACK, CHUNK], F32, name="pre", tag="early%d" % (len(made) % 4))
+            pre = psum.tile([P, PACK, CHUNK], F32, name="pre", tag="bank%d" % (len(made) % 4))
             made.append(pre)
             for t in range(PACK):
                 cols = slice(t * P, (t + 1) * P)
@@ -117,7 +117,7 @@ def tile_picked_yhnet_loss_p_kernel(
                 out=steep[:], in_=pre[:].rearrange("p t n -> p n t"), func=ACT.Tanh, scale=2.0
             )
             nc.vector.tensor_tensor(
-                out=grouped.rearrange("p (n t) -> p n t", t=PACK),
+                out=grouped[:, c * CHUNK * PACK : (c + 1) * CHUNK * PACK].rearrange("p (n t) -> p n t", t=PACK),
                 in0=steep[:],
                 in1=factor[:].unsqueeze(1).to_broadcast([P, CHUNK, PACK]),
                 op=ALU.mult,
@@ -131,114 +131,103 @@ def tile_picked_yhnet_loss_p_kernel(
         ha_scales = keep.tile([P, S], U8, name="ha_scales", align_bytes=64)
 
         def hidden_b(c):
-            hidden(xb_words, xb_scales, c, inv_sb, hb_grouped[:, c * CHUNK * PACK : (c + 1) * CHUNK * PACK])
+            hidden(xb_words, xb_scales, c, inv_sb, hb_grouped)
 
         def hidden_a(c):
-            hidden(xa_words, xa_scales, c, unit_sb, ha_grouped[:, c * CHUNK * PACK : (c + 1) * CHUNK * PACK])
+            hidden(xa_words, xa_scales, c, unit_sb, ha_grouped)
 
         def quantise(grouped, codes, scales, c0, c1):
             nc.vector.quantize_mx(
-                out=codes[:, c0:c1].bitcast(FP8X4),
-                scales=scales[:, c0:c1],
-                in_=grouped[:, c0 * PACK : c1 * PACK],
+                out=codes[:, c0 * CHUNK : c1 * CHUNK].bitcast(FP8X4),
+                scales=scales[:, c0 * CHUNK : c1 * CHUNK],
+                in_=grouped[:, c0 * CHUNK * PACK : c1 * CHUNK * PACK],
             )
 
-        blocks = []
+        groups = [(0, 2, 0, 2 * P), (0, 2, 2 * P, V), (2, 3, 0, V), (3, 4, 0, V)]
+        signed = keep.tile([P, S // P, V], F32, name="signed")
+        grown = keep.tile([P, S // P, V], F32, name="grown")
+        knees = keep.tile([P, 1], F32, name="knees")
+        nc.gpsimd.memset(knees[:], KNEE)
 
-        def score(k, t0, t1):
-            y = psum.tile([P, t1 - t0], F32, name="y", tag="score%d" % len(blocks))
-            rows = slice(k * CHUNK, (k + 1) * CHUNK)
-            nc.tensor.matmul_mx(
-                out=y[:],
-                lhsT=hb_codes[:, rows].bitcast(FP8X4),
-                lhsT_scale=hb_scales[:, rows],
-                rhs=ha_codes[:, t0:t1].bitcast(FP8X4),
-                rhs_scale=ha_scales[:, t0:t1],
-                start=True,
-                stop=True,
-            )
-            blocks.append((k, t0, t1, y))
-
-        for c in range(S // CHUNK):
-            hidden_a(c)
-        hidden_b(0)
-        quantise(ha_grouped, ha_codes, ha_scales, 0, S)
-        for k in range(V // CHUNK):
-            if 0 < k < V // CHUNK - 1:
-                hidden_b(k + 1)
-            quantise(hb_grouped, hb_codes, hb_scales, k * CHUNK, (k + 1) * CHUNK)
-            score(k, 0, S)
-            if k == 0:
-                hidden_b(1)
-
-        tiles = V // P
-        bent = keep.tile([P, tiles, S], F32, name="bent")
-        size = keep.tile([P, tiles, S], F32, name="size")
-        for k, t0, t1, y in blocks:
-            nc.scalar.activation(out=bent[:, k, t0:t1], in_=y[:], func=ACT.Tanh, scale=0.5)
-        for k in range(tiles - 2):
-            nc.scalar.activation(out=size[:, k, :], in_=bent[:, k, :], func=ACT.Abs)
-
-        slope = keep.tile([P, tiles, S], F32, name="slope")
-        slanted = keep.tile([P, tiles, S], F32, name="slanted")
-
-        def make_slope(k):
-            turned = psum.tile([P, S], F32, name="turned", tag="early%d" % k)
-            for i in range(S // P):
-                nc.tensor.transpose(turned[:, i * P : (i + 1) * P], sim_sb[:, i, k * P : (k + 1) * P], identity[:])
-            nc.vector.scalar_tensor_tensor(
-                out=slope[:, k, :], in0=bent[:, k, :], scalar=0.0, in1=turned[:], op0=ALU.is_gt, op1=ALU.subtract
-            )
-
-        def slant(k):
-            for kk, t0, t1, y in blocks:
-                if kk == k:
-                    nc.vector.scalar_tensor_tensor(
-                        out=slanted[:, k, t0:t1],
-                        in0=y[:],
-                        scalar=-1.0,
-                        in1=slope[:, k, t0:t1],
-                        op0=ALU.mult,
-                        op1=ALU.mult,
-                    )
-
-        make_slope(0)
-        for k in range(1, tiles):
-            if k == tiles - 2:
-                nc.vector.scalar_tensor_tensor(
-                    out=size[:, k, :], in0=bent[:, k, :], scalar=-1.0, in1=bent[:, k, :], op0=ALU.mult, op1=ALU.max
+        def score(g):
+            i0, i1, c0, c1 = groups[g]
+            y = psum.tile([P, i1 - i0, c1 - c0], F32, name="y", tag="bank%d" % (4 + g))
+            for i in range(i0, i1):
+                nc.tensor.matmul_mx(
+                    out=y[:, i - i0, :],
+                    lhsT=ha_codes[:, i * P : (i + 1) * P].bitcast(FP8X4),
+                    lhsT_scale=ha_scales[:, i * P : (i + 1) * P],
+                    rhs=hb_codes[:, c0:c1].bitcast(FP8X4),
+                    rhs_scale=hb_scales[:, c0:c1],
+                    start=True,
+                    stop=True,
                 )
-            make_slope(k)
-            slant(k - 1)
-        slant(tiles - 1)
+            return y
 
-        last = S // P - 1
-        parts = [(i, 0, tiles) for i in range(last)] + [(last, 0, tiles // 2), (last, tiles // 2, tiles)]
-        banks = ("early0", "early1", "score0", "early2", "score1")
-        losses = [
-            psum.tile([P, (k1 - k0) * P], F32, name="loss", tag=tag) for (i, k0, k1), tag in zip(parts, banks)
-        ]
+        def sign_and_grow(g, y, pieces):
+            i0, i1, c0, c1 = groups[g]
+            step = (c1 - c0) // pieces
+            for n in range(c0, c1, step):
+                cols = slice(n, n + step)
+                nc.vector.scalar_tensor_tensor(
+                    out=signed[:, i0:i1, cols],
+                    in0=sim_sb[:, i0:i1, cols],
+                    scalar=0.5,
+                    in1=y[:, :, n - c0 : n - c0 + step],
+                    op0=ALU.subtract,
+                    op1=ALU.mult,
+                )
+                room = ring.tile([P, i1 - i0, step], F32, name="room", bufs=4)
+                if g in (2, 3):
+                    nc.vector.tensor_scalar(
+                        out=room[:], in0=signed[:, i0:i1, cols], scalar1=2.0, scalar2=-KNEE, op0=ALU.mult, op1=ALU.max
+                    )
+                    nc.scalar.activation(out=grown[:, i0:i1, cols], in_=room[:], func=ACT.Exp, scale=-1.0, bias=zero[:])
+                else:
+                    nc.scalar.activation(out=room[:], in_=signed[:, i0:i1, cols], func=ACT.Relu, scale=2.0, bias=knees[:])
+                    nc.scalar.activation(out=grown[:, i0:i1, cols], in_=room[:], func=ACT.Exp, scale=-1.0, bias=knees[:])
 
-        def add_turned(loss, column, block, start, stop):
-            nc.tensor.matmul(
-                loss[:, column * P : (column + 1) * P], block, identity[:], start=start, stop=stop, is_transpose=True
-            )
+        zero = keep.tile([P, 1], F32, name="zero", tag="soft")
+        nc.gpsimd.memset(zero[:], 0.0)
+        hidden_b(0)
+        hidden_b(1)
+        hidden_a(0)
+        quantise(hb_grouped, hb_codes, hb_scales, 0, 2)
+        hidden_a(1)
+        quantise(ha_grouped, ha_codes, ha_scales, 0, 2)
+        y0 = score(0)
+        hidden_b(2)
+        hidden_b(3)
+        sign_and_grow(0, y0, 1)
+        quantise(hb_grouped, hb_codes, hb_scales, 2, 4)
+        y1 = score(1)
+        hidden_a(2)
+        quantise(ha_grouped, ha_codes, ha_scales, 2, 3)
+        y2 = score(2)
+        sign_and_grow(1, y1, 1)
+        hidden_a(3)
+        quantise(ha_grouped, ha_codes, ha_scales, 3, 4)
+        y3 = score(3)
+        sign_and_grow(2, y2, 1)
+        sign_and_grow(3, y3, 2)
 
-        for k in range(tiles):
-            for (i, k0, k1), loss in zip(parts, losses):
-                if k0 <= k < k1:
-                    add_turned(loss, k - k0, slanted[:, k, i * P : (i + 1) * P], k == k0, False)
-
-        for b, ((i, k0, k1), loss) in enumerate(zip(parts, losses)):
-            rows = slice(i * P, (i + 1) * P)
-            if k1 == tiles:
-                nc.scalar.activation(out=size[:, tiles - 1, rows], in_=bent[:, tiles - 1, rows], func=ACT.Abs)
-            soft = keep.tile([P, k1 - k0, P], F32, name="soft%d" % b, tag="soft%d" % (b % last))
-            nc.scalar.activation(out=soft[:], in_=size[:, k0:k1, rows], func=ACT.Ln, scale=0.5, bias=0.5)
-            for k in range(k0, k1):
-                add_turned(loss, k - k0, soft[:, k - k0, :], False, k == k1 - 1)
-            result = keep.tile([P, (k1 - k0) * P], F32, name="result%d" % b)
+        stretch = keep.tile([P, S // P, V], F32, name="stretch")
+        for i in range(S // P):
             nc.vector.scalar_tensor_tensor(
-                out=result[:], in0=loss[:], scalar=-1.0, in1=wt_sb[:, i, k0 * P : k1 * P], op0=ALU.mult, op1=ALU.mult
+                out=stretch[:, i, :],
+                in0=signed[:, i, :],
+                scalar=-0.5 * KNEE,
+                in1=wt_sb[:, i, :],
+                op0=ALU.min,
+                op1=ALU.mult,
             )
-            nc.sync.dma_start(out=out[rows, k0 * P : k1 * P], in_=result[:])
+
+        soft = keep.tile([P, 4, V], F32, name="soft", tag="soft")
+        for i, c0, c1 in ((0, 0, V), (1, 0, V), (2, 0, V), (3, 0, V // 2), (3, V // 2, V)):
+            logs = soft[:, i, c0:c1]
+            nc.scalar.activation(out=logs, in_=grown[:, i, c0:c1], func=ACT.Ln, bias=1.0)
+            result = keep.tile([P, c1 - c0], F32, name="result%d_%d" % (i, c0))
+            nc.vector.scalar_tensor_tensor(
+                out=result[:], in0=logs, scalar=-2.0 / KNEE, in1=stretch[:, i, c0:c1], op0=ALU.mult, op1=ALU.mult
+            )
+            nc.sync.dma_start(out=out[i * P : (i + 1) * P, c0:c1], in_=result[:])

@@ -1,3 +1,4 @@
+import math
 from contextlib import ExitStack
 
 import concourse.mybir as mybir
@@ -164,6 +165,8 @@ def tile_picked_yhnet_loss_p_kernel(
                 )
             return y
 
+        late = []
+
         def sign_and_grow(g, y, pieces):
             i0, i1, c0, c1 = groups[g]
             step = (c1 - c0) // pieces
@@ -178,11 +181,9 @@ def tile_picked_yhnet_loss_p_kernel(
                     op1=ALU.mult,
                 )
                 room = ring.tile([P, i1 - i0, step], F32, name="room", bufs=4)
-                if g in (2, 3):
-                    nc.vector.tensor_scalar(
-                        out=room[:], in0=signed[:, i0:i1, cols], scalar1=2.0, scalar2=-KNEE, op0=ALU.mult, op1=ALU.max
-                    )
-                    nc.scalar.activation(out=grown[:, i0:i1, cols], in_=room[:], func=ACT.Exp, scale=-1.0, bias=zero[:])
+                if g in (1, 2, 3):
+                    nc.scalar.activation(out=room[:], in_=signed[:, i0:i1, cols], func=ACT.Exp, scale=-2.0, bias=zero[:])
+                    late.append((room, grown[:, i0:i1, cols]))
                 else:
                     nc.scalar.activation(out=room[:], in_=signed[:, i0:i1, cols], func=ACT.Relu, scale=2.0, bias=knees[:])
                     nc.scalar.activation(out=grown[:, i0:i1, cols], in_=room[:], func=ACT.Exp, scale=-1.0, bias=knees[:])
@@ -210,6 +211,11 @@ def tile_picked_yhnet_loss_p_kernel(
         y3 = score(3)
         sign_and_grow(2, y2, 1)
         sign_and_grow(3, y3, 2)
+
+        room, dst = late[0]
+        nc.gpsimd.tensor_scalar(out=dst, in0=room[:], scalar1=math.exp(KNEE), scalar2=0.0, op0=ALU.min, op1=ALU.max)
+        for room, dst in late[1:]:
+            nc.vector.tensor_scalar_min(dst, room[:], math.exp(KNEE))
 
         stretch = keep.tile([P, S // P, V], F32, name="stretch")
         for i in range(S // P):

@@ -1,4 +1,3 @@
-import math
 from contextlib import ExitStack
 
 import concourse.mybir as mybir
@@ -20,7 +19,8 @@ P = 128
 PACK = 4
 CHUNK = 128
 GATHER = 256
-KNEE = 32.0
+KNEE = 16.0
+TINY = 2.0**-60
 
 
 def tile_picked_yhnet_loss_p_kernel(
@@ -70,6 +70,15 @@ def tile_picked_yhnet_loss_p_kernel(
         xa_scales = keep.tile([P, S], U8, name="xa_scales", align_bytes=64)
         nc.vector.tensor_copy(xb_scales[:], store_scales[:].indirect(list_b[:]))
         nc.vector.tensor_copy(xa_scales[:], store_scales[:].indirect(list_a[:]))
+
+        zero = keep.tile([P, 1], F32, name="zero", tag="logs")
+        nc.gpsimd.memset(zero[:], 0.0)
+        one_half = keep.tile([P, 1], F32, name="one_half")
+        nc.scalar.activation(out=one_half[:], in_=zero[:], func=ACT.Sigmoid)
+        unit_small = keep.tile([P, PACK], F32, name="unit_small")
+        nc.gpsimd.tensor_scalar(
+            out=unit_small[:], in0=unit_sb[:], scalar1=2.0 / KNEE, scalar2=0.0, op0=ALU.mult, op1=ALU.add
+        )
 
         w_grouped = keep.tile([P, H * PACK], BF16, name="w_grouped", align_bytes=64)
         w_dst = w_grouped[:].rearrange("p (t m j) -> p m j t", t=PACK, j=PACK)
@@ -135,7 +144,7 @@ def tile_picked_yhnet_loss_p_kernel(
             hidden(xb_words, xb_scales, c, inv_sb, hb_grouped)
 
         def hidden_a(c):
-            hidden(xa_words, xa_scales, c, unit_sb, ha_grouped)
+            hidden(xa_words, xa_scales, c, unit_small, ha_grouped)
 
         def quantise(grouped, codes, scales, c0, c1):
             nc.vector.quantize_mx(
@@ -146,9 +155,7 @@ def tile_picked_yhnet_loss_p_kernel(
 
         groups = [(0, 2, 0, 2 * P), (0, 2, 2 * P, V), (2, 3, 0, V), (3, 4, 0, V)]
         signed = keep.tile([P, S // P, V], F32, name="signed")
-        grown = keep.tile([P, S // P, V], F32, name="grown")
-        knees = keep.tile([P, 1], F32, name="knees")
-        nc.gpsimd.memset(knees[:], KNEE)
+        squashed = keep.tile([P, S // P, V], F32, name="squashed")
 
         def score(g):
             i0, i1, c0, c1 = groups[g]
@@ -165,9 +172,7 @@ def tile_picked_yhnet_loss_p_kernel(
                 )
             return y
 
-        late = []
-
-        def sign_and_grow(g, y, pieces):
+        def sign_and_squash(g, y, pieces):
             i0, i1, c0, c1 = groups[g]
             step = (c1 - c0) // pieces
             for n in range(c0, c1, step):
@@ -175,21 +180,15 @@ def tile_picked_yhnet_loss_p_kernel(
                 nc.vector.scalar_tensor_tensor(
                     out=signed[:, i0:i1, cols],
                     in0=sim_sb[:, i0:i1, cols],
-                    scalar=0.5,
+                    scalar=one_half[:],
                     in1=y[:, :, n - c0 : n - c0 + step],
                     op0=ALU.subtract,
                     op1=ALU.mult,
                 )
-                room = ring.tile([P, i1 - i0, step], F32, name="room", bufs=4)
-                if g in (1, 2, 3):
-                    nc.scalar.activation(out=room[:], in_=signed[:, i0:i1, cols], func=ACT.Exp, scale=-2.0, bias=zero[:])
-                    late.append((room, grown[:, i0:i1, cols]))
-                else:
-                    nc.scalar.activation(out=room[:], in_=signed[:, i0:i1, cols], func=ACT.Relu, scale=2.0, bias=knees[:])
-                    nc.scalar.activation(out=grown[:, i0:i1, cols], in_=room[:], func=ACT.Exp, scale=-1.0, bias=knees[:])
+                nc.scalar.activation(
+                    out=squashed[:, i0:i1, cols], in_=signed[:, i0:i1, cols], func=ACT.Sigmoid, scale=KNEE, bias=zero[:]
+                )
 
-        zero = keep.tile([P, 1], F32, name="zero", tag="soft")
-        nc.gpsimd.memset(zero[:], 0.0)
         hidden_b(0)
         hidden_b(1)
         hidden_a(0)
@@ -199,41 +198,36 @@ def tile_picked_yhnet_loss_p_kernel(
         y0 = score(0)
         hidden_b(2)
         hidden_b(3)
-        sign_and_grow(0, y0, 1)
+        sign_and_squash(0, y0, 1)
         quantise(hb_grouped, hb_codes, hb_scales, 2, 4)
         y1 = score(1)
         hidden_a(2)
         quantise(ha_grouped, ha_codes, ha_scales, 2, 3)
         y2 = score(2)
-        sign_and_grow(1, y1, 1)
+        sign_and_squash(1, y1, 1)
         hidden_a(3)
         quantise(ha_grouped, ha_codes, ha_scales, 3, 4)
         y3 = score(3)
-        sign_and_grow(2, y2, 1)
-        sign_and_grow(3, y3, 2)
-
-        room, dst = late[0]
-        nc.gpsimd.tensor_scalar(out=dst, in0=room[:], scalar1=math.exp(KNEE), scalar2=0.0, op0=ALU.min, op1=ALU.max)
-        for room, dst in late[1:]:
-            nc.vector.tensor_scalar_min(dst, room[:], math.exp(KNEE))
+        sign_and_squash(2, y2, 1)
+        sign_and_squash(3, y3, 2)
 
         stretch = keep.tile([P, S // P, V], F32, name="stretch")
         for i in range(S // P):
             nc.vector.scalar_tensor_tensor(
-                out=stretch[:, i, :],
-                in0=signed[:, i, :],
-                scalar=-0.5 * KNEE,
-                in1=wt_sb[:, i, :],
-                op0=ALU.min,
-                op1=ALU.mult,
+                out=stretch[:, i, :], in0=signed[:, i, :], scalar=-1.0, in1=wt_sb[:, i, :], op0=ALU.min, op1=ALU.mult
             )
 
-        soft = keep.tile([P, 4, V], F32, name="soft", tag="soft")
-        for i, c0, c1 in ((0, 0, V), (1, 0, V), (2, 0, V), (3, 0, V // 2), (3, V // 2, V)):
-            logs = soft[:, i, c0:c1]
-            nc.scalar.activation(out=logs, in_=grown[:, i, c0:c1], func=ACT.Ln, bias=1.0)
-            result = keep.tile([P, c1 - c0], F32, name="result%d_%d" % (i, c0))
+        logs = keep.tile([P, S // P, V], F32, name="logs", tag="logs")
+        results = keep.tile([P, S // P, V], F32, name="results")
+        for i, c0, c1, stored in [(i, c, c + 256, (V if i < 3 else 256) if c or i == 3 else 0) for i in range(4) for c in (0, 256)]:
+            nc.scalar.activation(out=logs[:, i, c0:c1], in_=squashed[:, i, c0:c1], func=ACT.Ln, bias=TINY)
             nc.vector.scalar_tensor_tensor(
-                out=result[:], in0=logs, scalar=-2.0 / KNEE, in1=stretch[:, i, c0:c1], op0=ALU.mult, op1=ALU.mult
+                out=results[:, i, c0:c1],
+                in0=logs[:, i, c0:c1],
+                scalar=-KNEE,
+                in1=stretch[:, i, c0:c1],
+                op0=ALU.max,
+                op1=ALU.mult,
             )
-            nc.sync.dma_start(out=out[i * P : (i + 1) * P, c0:c1], in_=result[:])
+            if stored:
+                nc.sync.dma_start(out=out[i * P : (i + 1) * P, c1 - stored : c1], in_=results[:, i, c1 - stored : c1])

@@ -1,6 +1,7 @@
 from contextlib import ExitStack
 
 import concourse.mybir as mybir
+from concourse.masks import make_identity
 
 K, T, S, H, V = 512, 2048, 512, 512, 512
 FLOPS = 2 * K * H * S + 2 * K * H * V + 2 * H * S * V
@@ -75,9 +76,12 @@ def tile_picked_yhnet_loss_p_kernel(
         nc.gpsimd.memset(zero[:], 0.0)
         one_half = keep.tile([P, 1], F32, name="one_half")
         nc.scalar.activation(out=one_half[:], in_=zero[:], func=ACT.Sigmoid)
-        unit_small = keep.tile([P, PACK], F32, name="unit_small")
+        identity = keep.tile([P, P], F32, name="identity")
+        make_identity(nc, identity[:])
+        unit_small = keep.tile([P, P], F32, name="unit_small")
+        nc.gpsimd.memset(unit_small[:], 0.0)
         nc.gpsimd.tensor_scalar(
-            out=unit_small[:], in0=unit_sb[:], scalar1=2.0 / KNEE, scalar2=0.0, op0=ALU.mult, op1=ALU.add
+            out=unit_small[:, 0:PACK], in0=unit_sb[:], scalar1=2.0 / KNEE, scalar2=0.0, op0=ALU.mult, op1=ALU.add
         )
 
         w_grouped = keep.tile([P, H * PACK], BF16, name="w_grouped", align_bytes=64)
@@ -106,7 +110,7 @@ def tile_picked_yhnet_loss_p_kernel(
 
         made = []
 
-        def hidden(pieces, scales, c, factor, grouped):
+        def hidden(pieces, scales, c, factor, dst, engine, tag):
             piece = pieces[c * CHUNK // GATHER]
             n0 = c * CHUNK % GATHER
             pre = psum.tile([P, PACK, CHUNK], F32, name="pre", tag="bank%d" % (len(made) % 4))
@@ -122,29 +126,31 @@ def tile_picked_yhnet_loss_p_kernel(
                     start=True,
                     stop=True,
                 )
-            steep = ring.tile([P, CHUNK, PACK], F32, name="steep", bufs=8)
+            steep = keep.tile([P, CHUNK, PACK], F32, name="steep", tag=tag, align_bytes=64)
             nc.scalar.activation(
                 out=steep[:], in_=pre[:].rearrange("p t n -> p n t"), func=ACT.Tanh, scale=2.0
             )
-            nc.vector.tensor_tensor(
-                out=grouped[:, c * CHUNK * PACK : (c + 1) * CHUNK * PACK].rearrange("p (n t) -> p n t", t=PACK),
+            engine.tensor_tensor(
+                out=dst.rearrange("p (n t) -> p n t", t=PACK),
                 in0=steep[:],
-                in1=factor[:].unsqueeze(1).to_broadcast([P, CHUNK, PACK]),
+                in1=factor[:, 0:PACK].unsqueeze(1).to_broadcast([P, CHUNK, PACK]),
                 op=ALU.mult,
             )
 
-        hb_grouped = keep.tile([P, V * PACK], BF16, name="hb_grouped", align_bytes=64)
-        hb_codes = keep.tile([P, V], U32, name="hb_codes", align_bytes=64)
+        hb_grouped = keep.tile([P, V * PACK], BF16, name="hb_grouped", tag="signed", align_bytes=64)
+        hb_codes = keep.tile([P, V // 2], U32, name="hb_codes", align_bytes=64)
         hb_scales = keep.tile([P, V], U8, name="hb_scales", align_bytes=64)
         ha_grouped = keep.tile([P, S * PACK], BF16, name="ha_grouped", align_bytes=64)
         ha_codes = keep.tile([P, S], U32, name="ha_codes", align_bytes=64)
         ha_scales = keep.tile([P, S], U8, name="ha_scales", align_bytes=64)
 
         def hidden_b(c):
-            hidden(xb_words, xb_scales, c, inv_sb, hb_grouped)
+            dst = hb_grouped[:, c * CHUNK * PACK : (c + 1) * CHUNK * PACK]
+            hidden(xb_words, xb_scales, c, inv_sb, dst, nc.vector, "steep_b%d" % c)
 
-        def hidden_a(c):
-            hidden(xa_words, xa_scales, c, unit_small, ha_grouped)
+        def hidden_a(c, factor):
+            dst = ha_grouped[:, c * CHUNK * PACK : (c + 1) * CHUNK * PACK]
+            hidden(xa_words, xa_scales, c, factor, dst, nc.vector, "steep_a%d" % c)
 
         def quantise(grouped, codes, scales, c0, c1):
             nc.vector.quantize_mx(
@@ -154,22 +160,23 @@ def tile_picked_yhnet_loss_p_kernel(
             )
 
         groups = [(0, 2, 0, 2 * P), (0, 2, 2 * P, V), (2, 3, 0, V), (3, 4, 0, V)]
-        signed = keep.tile([P, S // P, V], F32, name="signed")
+        hb_halves = [hb_codes]
         squashed = keep.tile([P, S // P, V], F32, name="squashed")
 
         def score(g):
             i0, i1, c0, c1 = groups[g]
             y = psum.tile([P, i1 - i0, c1 - c0], F32, name="y", tag="bank%d" % (4 + g))
             for i in range(i0, i1):
-                nc.tensor.matmul_mx(
-                    out=y[:, i - i0, :],
-                    lhsT=ha_codes[:, i * P : (i + 1) * P].bitcast(FP8X4),
-                    lhsT_scale=ha_scales[:, i * P : (i + 1) * P],
-                    rhs=hb_codes[:, c0:c1].bitcast(FP8X4),
-                    rhs_scale=hb_scales[:, c0:c1],
-                    start=True,
-                    stop=True,
-                )
+                for n in range(c0, c1, V // 2):
+                    nc.tensor.matmul_mx(
+                        out=y[:, i - i0, n - c0 : n - c0 + V // 2],
+                        lhsT=ha_codes[:, i * P : (i + 1) * P].bitcast(FP8X4),
+                        lhsT_scale=ha_scales[:, i * P : (i + 1) * P],
+                        rhs=hb_halves[2 * n // V][:].bitcast(FP8X4),
+                        rhs_scale=hb_scales[:, n : n + V // 2],
+                        start=True,
+                        stop=True,
+                    )
             return y
 
         def sign_and_squash(g, y, pieces):
@@ -191,23 +198,39 @@ def tile_picked_yhnet_loss_p_kernel(
 
         hidden_b(0)
         hidden_b(1)
-        hidden_a(0)
+        hidden_a(0, unit_small)
         quantise(hb_grouped, hb_codes, hb_scales, 0, 2)
-        hidden_a(1)
+        hidden_a(1, unit_small)
         quantise(ha_grouped, ha_codes, ha_scales, 0, 2)
         y0 = score(0)
+
+        unit_rows = psum.tile([P, P], F32, name="unit_rows", tag="bank6")
+        nc.tensor.transpose(unit_rows[:], unit_small[:], identity[:])
+        rows_sb = keep.tile([P, P], F32, name="rows_sb")
+        nc.scalar.copy(rows_sb[:], unit_rows[:])
+        unit_ps = psum.tile([P, P], F32, name="unit_ps", tag="bank7")
+        nc.tensor.transpose(unit_ps[:], rows_sb[:], identity[:])
+
         hidden_b(2)
-        hidden_b(3)
-        sign_and_squash(0, y0, 1)
-        quantise(hb_grouped, hb_codes, hb_scales, 2, 4)
+        b_last = keep.tile([P, CHUNK * PACK], BF16, name="b_last", tag="steep_b2", align_bytes=64)
+        hidden(xb_words, xb_scales, 3, inv_sb, b_last[:], nc.gpsimd, "steep_b3")
+        hidden_a(2, unit_ps)
+        hidden_a(3, unit_ps)
+        hb_late = keep.tile([P, V // 2], U32, name="hb_late", tag="steep_b3", align_bytes=64)
+        hb_halves.append(hb_late)
+        nc.vector.quantize_mx(out=hb_late[:, P:].bitcast(FP8X4), scales=hb_scales[:, 3 * P :], in_=b_last[:])
+        nc.vector.quantize_mx(
+            out=hb_late[:, 0:P].bitcast(FP8X4),
+            scales=hb_scales[:, 2 * P : 3 * P],
+            in_=hb_grouped[:, 2 * CHUNK * PACK : 3 * CHUNK * PACK],
+        )
         y1 = score(1)
-        hidden_a(2)
-        quantise(ha_grouped, ha_codes, ha_scales, 2, 3)
+        quantise(ha_grouped, ha_codes, ha_scales, 2, 4)
         y2 = score(2)
-        sign_and_squash(1, y1, 1)
-        hidden_a(3)
-        quantise(ha_grouped, ha_codes, ha_scales, 3, 4)
         y3 = score(3)
+        signed = keep.tile([P, S // P, V], F32, name="signed", tag="signed", align_bytes=64)
+        sign_and_squash(0, y0, 1)
+        sign_and_squash(1, y1, 1)
         sign_and_squash(2, y2, 1)
         sign_and_squash(3, y3, 2)
 

@@ -229,9 +229,9 @@ def tile_picked_yhnet_loss_p_kernel(
         y2 = score(2)
         y3 = score(3)
         signed = keep.tile([P, S // P, V], F32, name="signed", tag="signed", align_bytes=64)
-        sign_and_squash(0, y0, 1)
-        sign_and_squash(1, y1, 1)
-        sign_and_squash(2, y2, 1)
+        sign_and_squash(0, y0, 2)
+        sign_and_squash(1, y1, 2)
+        sign_and_squash(2, y2, 2)
         sign_and_squash(3, y3, 2)
 
         stretch = keep.tile([P, S // P, V], F32, name="stretch")

@@ -30,7 +30,6 @@ def tile_picked_yhnet_loss_p_kernel(
     nc = tc.nc
     with ExitStack() as ctx:
         keep = ctx.enter_context(tc.tile_pool(name="keep", bufs=1))
-        ring = ctx.enter_context(tc.tile_pool(name="ring", bufs=4))
         psum = ctx.enter_context(tc.psum_pool(name="psum", bufs=1))
 
         list_b = keep.tile([P, V // 16], U16, name="list_b")
@@ -99,8 +98,10 @@ def tile_picked_yhnet_loss_p_kernel(
 
         def gather_words(name, offsets, g):
             piece = keep.tile([P, GATHER], U32, name="%s%d" % (name, g), align_bytes=64)
-            cols = slice(g * GATHER // 16, (g + 1) * GATHER // 16)
-            nc.vector.tensor_copy(piece[:], store_words[:].bitcast(U32).indirect(offsets[:, cols]))
+            step = CHUNK if name == "xb_words" and g == 0 else GATHER
+            for n in range(0, GATHER, step):
+                cols = slice((g * GATHER + n) // 16, (g * GATHER + n + step) // 16)
+                nc.vector.tensor_copy(piece[:, n : n + step], store_words[:].bitcast(U32).indirect(offsets[:, cols]))
             return piece
 
         xb_words, xa_words = [], []

@@ -35,9 +35,14 @@ def tile_picked_yhnet_loss_p_kernel(
         list_b = keep.tile([P, V // 16], U16, name="list_b")
         list_a = keep.tile([P, S // 16], U16, name="list_a")
         nc.sync.dma_start(list_b[:], other)
+        nc.sync.dma_start(list_a[:], offs)
+        zero = keep.tile([P, 1], F32, name="zero", tag="logs")
+        nc.gpsimd.memset(zero[:], 0.0)
 
         store_scales = keep.tile([P, T], U8, name="store_scales", align_bytes=64)
         nc.vector.memset(store_scales[:].bitcast(I32), 0)
+        unit_row = keep.tile([P, H], F32, name="unit_row")
+        nc.vector.memset(unit_row[:], 0.0)
 
         w_rows = w1.rearrange("(p j) c -> p j c", j=PACK)
         w_raw = []
@@ -46,21 +51,19 @@ def tile_picked_yhnet_loss_p_kernel(
             nc.sync.dma_start(out=raw[:], in_=w_rows[:, :, h * H // 2 : (h + 1) * H // 2])
             w_raw.append(raw)
             if h == 0:
-                nc.sync.dma_start(list_a[:], offs)
                 for q in range(4):
                     nc.sync.dma_start(
                         out=store_scales[q:P:32, :].bitcast(I32),
                         in_=x_scales[0, q:16:4, :].bitcast(I32),
                     )
+        nc.sync.dma_start(out=unit_row[0:1, :], in_=unit.rearrange("h o -> o h"))
         store_words = keep.tile([P, T], I32, name="store_words", align_bytes=64)
         nc.sync.dma_start(
             out=store_words[:],
             in_=x_words[0].rearrange("p n r -> p (n r)").bitcast(I32),
         )
         inv_sb = keep.tile([P, PACK], F32, name="inv_sb")
-        unit_sb = keep.tile([P, PACK], F32, name="unit_sb")
         nc.sync.dma_start(out=inv_sb[:], in_=inv.rearrange("(p j) o -> p (j o)", j=PACK))
-        nc.sync.dma_start(out=unit_sb[:], in_=unit.rearrange("(p j) o -> p (j o)", j=PACK))
         sim_sb = keep.tile([P, S // P, V], F32, name="sim_sb")
         wt_sb = keep.tile([P, S // P, V], F32, name="wt_sb")
         nc.sync.dma_start(out=sim_sb[:], in_=sim.rearrange("(i p) v -> p i v", p=P))
@@ -71,17 +74,13 @@ def tile_picked_yhnet_loss_p_kernel(
         nc.vector.tensor_copy(xb_scales[:], store_scales[:].indirect(list_b[:]))
         nc.vector.tensor_copy(xa_scales[:], store_scales[:].indirect(list_a[:]))
 
-        zero = keep.tile([P, 1], F32, name="zero", tag="logs")
-        nc.gpsimd.memset(zero[:], 0.0)
         one_half = keep.tile([P, 1], F32, name="one_half")
         nc.scalar.activation(out=one_half[:], in_=zero[:], func=ACT.Sigmoid)
         identity = keep.tile([P, P], F32, name="identity")
         make_identity(nc, identity[:])
-        unit_small = keep.tile([P, P], F32, name="unit_small")
-        nc.gpsimd.memset(unit_small[:], 0.0)
-        nc.gpsimd.tensor_scalar(
-            out=unit_small[:, 0:PACK], in0=unit_sb[:], scalar1=2.0 / KNEE, scalar2=0.0, op0=ALU.mult, op1=ALU.add
-        )
+        unit_ps = psum.tile([P, PACK, P], F32, name="unit_ps", tag="bank7")
+        for t in range(PACK):
+            nc.tensor.transpose(unit_ps[:, t, :], unit_row[:, t:H:PACK], identity[:])
 
         w_grouped = keep.tile([P, H * PACK], BF16, name="w_grouped", align_bytes=64)
         w_dst = w_grouped[:].rearrange("p (t m j) -> p m j t", t=PACK, j=PACK)
@@ -131,12 +130,14 @@ def tile_picked_yhnet_loss_p_kernel(
             nc.scalar.activation(
                 out=steep[:], in_=pre[:].rearrange("p t n -> p n t"), func=ACT.Tanh, scale=2.0
             )
-            engine.tensor_tensor(
-                out=dst.rearrange("p (n t) -> p n t", t=PACK),
-                in0=steep[:],
-                in1=factor[:, 0:PACK].unsqueeze(1).to_broadcast([P, CHUNK, PACK]),
-                op=ALU.mult,
-            )
+            rounded = dst.rearrange("p (n t) -> p n t", t=PACK)
+            spread = factor.unsqueeze(1).to_broadcast([P, CHUNK, PACK])
+            if pieces is xa_words:
+                engine.scalar_tensor_tensor(
+                    out=rounded, in0=steep[:], scalar=2.0 / KNEE, in1=spread, op0=ALU.mult, op1=ALU.mult
+                )
+            else:
+                engine.tensor_tensor(out=rounded, in0=steep[:], in1=spread, op=ALU.mult)
 
         hb_grouped = keep.tile([P, V * PACK], BF16, name="hb_grouped", tag="signed", align_bytes=64)
         hb_codes = keep.tile([P, V // 2], U32, name="hb_codes", align_bytes=64)
@@ -147,11 +148,11 @@ def tile_picked_yhnet_loss_p_kernel(
 
         def hidden_b(c):
             dst = hb_grouped[:, c * CHUNK * PACK : (c + 1) * CHUNK * PACK]
-            hidden(xb_words, xb_scales, c, inv_sb, dst, nc.vector, "steep_b%d" % c)
+            hidden(xb_words, xb_scales, c, inv_sb[:], dst, nc.vector, "steep_b%d" % c)
 
-        def hidden_a(c, factor):
+        def hidden_a(c):
             dst = ha_grouped[:, c * CHUNK * PACK : (c + 1) * CHUNK * PACK]
-            hidden(xa_words, xa_scales, c, factor, dst, nc.vector, "steep_a%d" % c)
+            hidden(xa_words, xa_scales, c, unit_ps[:, :, 0], dst, nc.vector, "steep_a%d" % c)
 
         def quantise(grouped, codes, scales, c0, c1):
             nc.vector.quantize_mx(
@@ -199,24 +200,17 @@ def tile_picked_yhnet_loss_p_kernel(
 
         hidden_b(0)
         hidden_b(1)
-        hidden_a(0, unit_small)
+        hidden_a(0)
         quantise(hb_grouped, hb_codes, hb_scales, 0, 2)
-        hidden_a(1, unit_small)
+        hidden_a(1)
         quantise(ha_grouped, ha_codes, ha_scales, 0, 2)
         y0 = score(0)
 
-        unit_rows = psum.tile([P, P], F32, name="unit_rows", tag="bank6")
-        nc.tensor.transpose(unit_rows[:], unit_small[:], identity[:])
-        rows_sb = keep.tile([P, P], F32, name="rows_sb")
-        nc.scalar.copy(rows_sb[:], unit_rows[:])
-        unit_ps = psum.tile([P, P], F32, name="unit_ps", tag="bank7")
-        nc.tensor.transpose(unit_ps[:], rows_sb[:], identity[:])
-
         hidden_b(2)
         b_last = keep.tile([P, CHUNK * PACK], BF16, name="b_last", tag="steep_b2", align_bytes=64)
-        hidden(xb_words, xb_scales, 3, inv_sb, b_last[:], nc.gpsimd, "steep_b3")
-        hidden_a(2, unit_ps)
-        hidden_a(3, unit_ps)
+        hidden(xb_words, xb_scales, 3, inv_sb[:], b_last[:], nc.gpsimd, "steep_b3")
+        hidden_a(2)
+        hidden_a(3)
         hb_late = keep.tile([P, V // 2], U32, name="hb_late", tag="steep_b3", align_bytes=64)
         hb_halves.append(hb_late)
         nc.vector.quantize_mx(out=hb_late[:, P:].bitcast(FP8X4), scales=hb_scales[:, 3 * P :], in_=b_last[:])

@@ -19,7 +19,8 @@ ALU = mybir.AluOpType
 P = 128
 PACK = 4
 CHUNK = 128
-GATHER = 256
+PAIR = 2 * CHUNK
+LANES = 16
 KNEE = 16.0
 TINY = 2.0**-60
 
@@ -32,10 +33,11 @@ def tile_picked_yhnet_loss_p_kernel(
         keep = ctx.enter_context(tc.tile_pool(name="keep", bufs=1))
         psum = ctx.enter_context(tc.psum_pool(name="psum", bufs=1))
 
-        list_b = keep.tile([P, V // 16], U16, name="list_b")
-        list_a = keep.tile([P, S // 16], U16, name="list_a")
+        list_b = keep.tile([P, V // LANES], U16, name="list_b")
+        list_a = keep.tile([P, S // LANES], U16, name="list_a")
         nc.sync.dma_start(list_b[:], other)
         nc.sync.dma_start(list_a[:], offs)
+
         zero = keep.tile([P, 1], F32, name="zero", tag="logs")
         nc.gpsimd.memset(zero[:], 0.0)
 
@@ -51,10 +53,10 @@ def tile_picked_yhnet_loss_p_kernel(
             nc.sync.dma_start(out=raw[:], in_=w_rows[:, :, h * H // 2 : (h + 1) * H // 2])
             w_raw.append(raw)
             if h == 0:
-                for q in range(4):
+                for r in range(4):
                     nc.sync.dma_start(
-                        out=store_scales[q:P:32, :].bitcast(I32),
-                        in_=x_scales[0, q:16:4, :].bitcast(I32),
+                        out=store_scales[r:P:32, :].bitcast(I32),
+                        in_=x_scales[0, r:16:4, :].bitcast(I32),
                     )
         nc.sync.dma_start(out=unit_row[0:1, :], in_=unit.rearrange("h o -> o h"))
         store_words = keep.tile([P, T], I32, name="store_words", align_bytes=64)
@@ -78,16 +80,16 @@ def tile_picked_yhnet_loss_p_kernel(
         nc.scalar.activation(out=one_half[:], in_=zero[:], func=ACT.Sigmoid)
         identity = keep.tile([P, P], F32, name="identity")
         make_identity(nc, identity[:])
+
         unit_ps = psum.tile([P, PACK, P], F32, name="unit_ps", tag="bank7")
         for t in range(PACK):
             nc.tensor.transpose(unit_ps[:, t, :], unit_row[:, t:H:PACK], identity[:])
 
         w_grouped = keep.tile([P, H * PACK], BF16, name="w_grouped", align_bytes=64)
         w_dst = w_grouped[:].rearrange("p (t m j) -> p m j t", t=PACK, j=PACK)
-        half = P // 2
         for h in range(2):
             nc.scalar.activation(
-                out=w_dst[:, h * half : (h + 1) * half],
+                out=w_dst[:, h * P // 2 : (h + 1) * P // 2],
                 in_=w_raw[h][:].rearrange("p j (m t) -> p m j t", t=PACK),
                 func=ACT.Copy,
             )
@@ -95,139 +97,128 @@ def tile_picked_yhnet_loss_p_kernel(
         w_scales = keep.tile([P, H], U8, name="w_scales", align_bytes=64)
         nc.vector.quantize_mx(out=w_codes[:].bitcast(FP8X4), scales=w_scales[:], in_=w_grouped[:])
 
-        def gather_words(name, offsets, g):
-            piece = keep.tile([P, GATHER], U32, name="%s%d" % (name, g), align_bytes=64)
-            step = CHUNK if name == "xb_words" and g == 0 else GATHER
-            for n in range(0, GATHER, step):
-                cols = slice((g * GATHER + n) // 16, (g * GATHER + n + step) // 16)
-                nc.vector.tensor_copy(piece[:, n : n + step], store_words[:].bitcast(U32).indirect(offsets[:, cols]))
-            return piece
+        def gather_words(name, offsets, g, step):
+            picked = keep.tile([P, PAIR], U32, name="%s%d" % (name, g), align_bytes=64)
+            for n in range(0, PAIR, step):
+                cols = slice((g * PAIR + n) // LANES, (g * PAIR + n + step) // LANES)
+                nc.vector.tensor_copy(picked[:, n : n + step], store_words[:].bitcast(U32).indirect(offsets[:, cols]))
+            return picked
 
         xb_words, xa_words = [], []
-        for g in range(S // GATHER):
-            xb_words.append(gather_words("xb_words", list_b, g))
-            xa_words.append(gather_words("xa_words", list_a, g))
+        for g in range(S // PAIR):
+            xb_words.append(gather_words("xb_words", list_b, g, PAIR if g else CHUNK))
+            xa_words.append(gather_words("xa_words", list_a, g, PAIR))
 
-        made = []
+        first_products = []
 
-        def hidden(pieces, scales, c, factor, dst, engine, tag):
-            piece = pieces[c * CHUNK // GATHER]
-            n0 = c * CHUNK % GATHER
-            pre = psum.tile([P, PACK, CHUNK], F32, name="pre", tag="bank%d" % (len(made) % 4))
-            made.append(pre)
+        def steep_tanh(side, c):
+            words, scales = (xa_words, xa_scales) if side == "a" else (xb_words, xb_scales)
+            n0 = c * CHUNK % PAIR
+            pre = psum.tile([P, PACK, CHUNK], F32, name="pre", tag="bank%d" % (len(first_products) % 4))
+            first_products.append(pre)
             for t in range(PACK):
                 cols = slice(t * P, (t + 1) * P)
                 nc.tensor.matmul_mx(
                     out=pre[:, t, :],
                     lhsT=w_codes[:, cols].bitcast(FP8X4),
                     lhsT_scale=w_scales[:, cols],
-                    rhs=piece[:, n0 : n0 + CHUNK].bitcast(FP8X4),
+                    rhs=words[c * CHUNK // PAIR][:, n0 : n0 + CHUNK].bitcast(FP8X4),
                     rhs_scale=scales[:, c * CHUNK : (c + 1) * CHUNK],
                     start=True,
                     stop=True,
                 )
-            steep = keep.tile([P, CHUNK, PACK], F32, name="steep", tag=tag, align_bytes=64)
+            steep = keep.tile([P, CHUNK, PACK], F32, name="steep", tag="steep_%s%d" % (side, c), align_bytes=64)
             nc.scalar.activation(
                 out=steep[:], in_=pre[:].rearrange("p t n -> p n t"), func=ACT.Tanh, scale=2.0
             )
-            rounded = dst.rearrange("p (n t) -> p n t", t=PACK)
-            spread = factor.unsqueeze(1).to_broadcast([P, CHUNK, PACK])
-            if pieces is xa_words:
-                engine.scalar_tensor_tensor(
-                    out=rounded, in0=steep[:], scalar=2.0 / KNEE, in1=spread, op0=ALU.mult, op1=ALU.mult
-                )
-            else:
-                engine.tensor_tensor(out=rounded, in0=steep[:], in1=spread, op=ALU.mult)
+            return steep
 
-        hb_grouped = keep.tile([P, V * PACK], BF16, name="hb_grouped", tag="signed", align_bytes=64)
-        hb_codes = keep.tile([P, V // 2], U32, name="hb_codes", align_bytes=64)
-        hb_scales = keep.tile([P, V], U8, name="hb_scales", align_bytes=64)
-        ha_grouped = keep.tile([P, S * PACK], BF16, name="ha_grouped", align_bytes=64)
-        ha_codes = keep.tile([P, S], U32, name="ha_codes", align_bytes=64)
-        ha_scales = keep.tile([P, S], U8, name="ha_scales", align_bytes=64)
+        def chunks(rounded, c0, c1):
+            return rounded[:, c0 * CHUNK * PACK : c1 * CHUNK * PACK]
 
-        def hidden_b(c):
-            dst = hb_grouped[:, c * CHUNK * PACK : (c + 1) * CHUNK * PACK]
-            hidden(xb_words, xb_scales, c, inv_sb[:], dst, nc.vector, "steep_b%d" % c)
-
-        def hidden_a(c):
-            dst = ha_grouped[:, c * CHUNK * PACK : (c + 1) * CHUNK * PACK]
-            hidden(xa_words, xa_scales, c, unit_ps[:, :, 0], dst, nc.vector, "steep_a%d" % c)
-
-        def quantise(grouped, codes, scales, c0, c1):
-            nc.vector.quantize_mx(
-                out=codes[:, c0 * CHUNK : c1 * CHUNK].bitcast(FP8X4),
-                scales=scales[:, c0 * CHUNK : c1 * CHUNK],
-                in_=grouped[:, c0 * CHUNK * PACK : c1 * CHUNK * PACK],
+        def hidden_b(c, dst, engine):
+            engine.tensor_tensor(
+                out=dst.rearrange("p (n t) -> p n t", t=PACK),
+                in0=steep_tanh("b", c)[:],
+                in1=inv_sb[:].unsqueeze(1).to_broadcast([P, CHUNK, PACK]),
+                op=ALU.mult,
             )
 
-        groups = [(0, 2, 0, 2 * P), (0, 2, 2 * P, V), (2, 3, 0, V), (3, 4, 0, V)]
-        hb_halves = [hb_codes]
+        def hidden_a(c):
+            nc.vector.scalar_tensor_tensor(
+                out=chunks(ha_rounded, c, c + 1).rearrange("p (n t) -> p n t", t=PACK),
+                in0=steep_tanh("a", c)[:],
+                scalar=2.0 / KNEE,
+                in1=unit_ps[:, :, 0].unsqueeze(1).to_broadcast([P, CHUNK, PACK]),
+                op0=ALU.mult,
+                op1=ALU.mult,
+            )
+
+        def quantise(codes, scales, rounded):
+            nc.vector.quantize_mx(out=codes.bitcast(FP8X4), scales=scales, in_=rounded)
+
+        hb_rounded = keep.tile([P, V * PACK], BF16, name="hb_rounded", align_bytes=64)
+        hb_early = keep.tile([P, PAIR], U32, name="hb_early", align_bytes=64)
+        hb_scales = keep.tile([P, V], U8, name="hb_scales", align_bytes=64)
+        ha_rounded = keep.tile([P, S * PACK], BF16, name="ha_rounded", align_bytes=64)
+        ha_codes = keep.tile([P, S], U32, name="ha_codes", align_bytes=64)
+        ha_scales = keep.tile([P, S], U8, name="ha_scales", align_bytes=64)
+        hb_codes = [hb_early]
+        signed = keep.tile([P, S // P, V], F32, name="signed")
         squashed = keep.tile([P, S // P, V], F32, name="squashed")
 
-        def score(g):
-            i0, i1, c0, c1 = groups[g]
-            y = psum.tile([P, i1 - i0, c1 - c0], F32, name="y", tag="bank%d" % (4 + g))
-            for i in range(i0, i1):
-                for n in range(c0, c1, V // 2):
-                    nc.tensor.matmul_mx(
-                        out=y[:, i - i0, n - c0 : n - c0 + V // 2],
-                        lhsT=ha_codes[:, i * P : (i + 1) * P].bitcast(FP8X4),
-                        lhsT_scale=ha_scales[:, i * P : (i + 1) * P],
-                        rhs=hb_halves[2 * n // V][:].bitcast(FP8X4),
-                        rhs_scale=hb_scales[:, n : n + V // 2],
-                        start=True,
-                        stop=True,
-                    )
-            return y
+        def score(i, u, bank):
+            y = psum.tile([P, PAIR], F32, name="y", tag="bank%d" % bank)
+            nc.tensor.matmul_mx(
+                out=y[:],
+                lhsT=ha_codes[:, i * P : (i + 1) * P].bitcast(FP8X4),
+                lhsT_scale=ha_scales[:, i * P : (i + 1) * P],
+                rhs=hb_codes[u][:].bitcast(FP8X4),
+                rhs_scale=hb_scales[:, u * PAIR : (u + 1) * PAIR],
+                start=True,
+                stop=True,
+            )
+            return i, u, y
 
-        def sign_and_squash(g, y, pieces):
-            i0, i1, c0, c1 = groups[g]
-            step = (c1 - c0) // pieces
-            for n in range(c0, c1, step):
-                cols = slice(n, n + step)
-                nc.vector.scalar_tensor_tensor(
-                    out=signed[:, i0:i1, cols],
-                    in0=sim_sb[:, i0:i1, cols],
-                    scalar=one_half[:],
-                    in1=y[:, :, n - c0 : n - c0 + step],
-                    op0=ALU.subtract,
-                    op1=ALU.mult,
-                )
-                nc.scalar.activation(
-                    out=squashed[:, i0:i1, cols], in_=signed[:, i0:i1, cols], func=ACT.Sigmoid, scale=KNEE, bias=zero[:]
-                )
+        def sign_and_squash(i, u, y):
+            cols = slice(u * PAIR, (u + 1) * PAIR)
+            nc.vector.scalar_tensor_tensor(
+                out=signed[:, i, cols],
+                in0=sim_sb[:, i, cols],
+                scalar=one_half[:],
+                in1=y[:],
+                op0=ALU.subtract,
+                op1=ALU.mult,
+            )
+            nc.scalar.activation(
+                out=squashed[:, i, cols], in_=signed[:, i, cols], func=ACT.Sigmoid, scale=KNEE, bias=zero[:]
+            )
 
-        hidden_b(0)
-        hidden_b(1)
+        hidden_b(0, chunks(hb_rounded, 0, 1), nc.vector)
+        hidden_b(1, chunks(hb_rounded, 1, 2), nc.vector)
         hidden_a(0)
-        quantise(hb_grouped, hb_codes, hb_scales, 0, 2)
+        quantise(hb_early[:], hb_scales[:, 0:PAIR], chunks(hb_rounded, 0, 2))
         hidden_a(1)
-        quantise(ha_grouped, ha_codes, ha_scales, 0, 2)
-        y0 = score(0)
+        quantise(ha_codes[:, 0:PAIR], ha_scales[:, 0:PAIR], chunks(ha_rounded, 0, 2))
+        first_piece = score(0, 0, 4)
 
-        hidden_b(2)
-        b_last = keep.tile([P, CHUNK * PACK], BF16, name="b_last", tag="steep_b2", align_bytes=64)
-        hidden(xb_words, xb_scales, 3, inv_sb[:], b_last[:], nc.gpsimd, "steep_b3")
+        hidden_b(2, chunks(hb_rounded, 2, 3), nc.vector)
+        hb_last = keep.tile([P, CHUNK * PACK], BF16, name="hb_last", tag="steep_b2", align_bytes=64)
+        hidden_b(3, hb_last[:], nc.gpsimd)
         hidden_a(2)
         hidden_a(3)
-        hb_late = keep.tile([P, V // 2], U32, name="hb_late", tag="steep_b3", align_bytes=64)
-        hb_halves.append(hb_late)
-        nc.vector.quantize_mx(out=hb_late[:, P:].bitcast(FP8X4), scales=hb_scales[:, 3 * P :], in_=b_last[:])
-        nc.vector.quantize_mx(
-            out=hb_late[:, 0:P].bitcast(FP8X4),
-            scales=hb_scales[:, 2 * P : 3 * P],
-            in_=hb_grouped[:, 2 * CHUNK * PACK : 3 * CHUNK * PACK],
-        )
-        y1 = score(1)
-        quantise(ha_grouped, ha_codes, ha_scales, 2, 4)
-        y2 = score(2)
-        y3 = score(3)
-        signed = keep.tile([P, S // P, V], F32, name="signed", tag="signed", align_bytes=64)
-        sign_and_squash(0, y0, 2)
-        sign_and_squash(1, y1, 2)
-        sign_and_squash(2, y2, 2)
-        sign_and_squash(3, y3, 2)
+        sign_and_squash(*first_piece)
+
+        pieces = [score(1, 0, 7)]
+        hb_late = keep.tile([P, PAIR], U32, name="hb_late", tag="steep_b3", align_bytes=64)
+        hb_codes.append(hb_late)
+        quantise(hb_late[:, CHUNK:], hb_scales[:, 3 * CHUNK :], hb_last[:])
+        quantise(hb_late[:, 0:CHUNK], hb_scales[:, PAIR : 3 * CHUNK], chunks(hb_rounded, 2, 3))
+        pieces.extend(score(i, 1, 5 + i) for i in range(2))
+        quantise(ha_codes[:, PAIR:], ha_scales[:, PAIR:], chunks(ha_rounded, 2, 4))
+        pieces.extend(score(i, u, 2 * (i - 2) + u) for i in range(2, 4) for u in range(2))
+        for piece in pieces:
+            sign_and_squash(*piece)
 
         stretch = keep.tile([P, S // P, V], F32, name="stretch")
         for i in range(S // P):
@@ -237,15 +228,21 @@ def tile_picked_yhnet_loss_p_kernel(
 
         logs = keep.tile([P, S // P, V], F32, name="logs", tag="logs")
         results = keep.tile([P, S // P, V], F32, name="results")
-        for i, c0, c1, stored in [(i, c, c + 256, (V if i < 3 else 256) if c or i == 3 else 0) for i in range(4) for c in (0, 256)]:
-            nc.scalar.activation(out=logs[:, i, c0:c1], in_=squashed[:, i, c0:c1], func=ACT.Ln, bias=TINY)
-            nc.vector.scalar_tensor_tensor(
-                out=results[:, i, c0:c1],
-                in0=logs[:, i, c0:c1],
-                scalar=-KNEE,
-                in1=stretch[:, i, c0:c1],
-                op0=ALU.max,
-                op1=ALU.mult,
-            )
-            if stored:
-                nc.sync.dma_start(out=out[i * P : (i + 1) * P, c1 - stored : c1], in_=results[:, i, c1 - stored : c1])
+        last = S // P - 1
+        for i in range(S // P):
+            rows = slice(i * P, (i + 1) * P)
+            for c0 in range(0, V, PAIR):
+                cols = slice(c0, c0 + PAIR)
+                nc.scalar.activation(out=logs[:, i, cols], in_=squashed[:, i, cols], func=ACT.Ln, bias=TINY)
+                nc.vector.scalar_tensor_tensor(
+                    out=results[:, i, cols],
+                    in0=logs[:, i, cols],
+                    scalar=-KNEE,
+                    in1=stretch[:, i, cols],
+                    op0=ALU.max,
+                    op1=ALU.mult,
+                )
+                if i == last:
+                    nc.sync.dma_start(out=out[rows, cols], in_=results[:, i, cols])
+            if i < last:
+                nc.sync.dma_start(out=out[rows, :], in_=results[:, i, :])

from contextlib import ExitStack

import concourse.mybir as mybir
from concourse.masks import make_identity

K, T, S, H, V = 512, 2048, 512, 512, 512
FLOPS = 2 * K * H * S + 2 * K * H * V + 2 * H * S * V

F32 = mybir.dt.float32
BF16 = mybir.dt.bfloat16
I32 = mybir.dt.int32
U32 = mybir.dt.uint32
U16 = mybir.dt.uint16
U8 = mybir.dt.uint8
FP8X4 = mybir.dt.float8_e4m3fn_x4
ACT = mybir.ActivationFunctionType
ALU = mybir.AluOpType

P = 128
PACK = 4
CHUNK = 128
PAIR = 2 * CHUNK
LANES = 16
KNEE = 16.0
TINY = 2.0**-60


def tile_picked_yhnet_loss_p_kernel(
    tc, x_words, x_scales, w1, unit, inv, sim, wt, offs, other, out
):
    nc = tc.nc
    with ExitStack() as ctx:
        keep = ctx.enter_context(tc.tile_pool(name="keep", bufs=1))
        psum = ctx.enter_context(tc.psum_pool(name="psum", bufs=1))

        list_b = keep.tile([P, V // LANES], U16, name="list_b")
        list_a = keep.tile([P, S // LANES], U16, name="list_a")
        nc.sync.dma_start(list_b[:], other)
        nc.sync.dma_start(list_a[:], offs)

        zero = keep.tile([P, 1], F32, name="zero", tag="logs")
        nc.gpsimd.memset(zero[:], 0.0)

        store_scales = keep.tile([P, T], U8, name="store_scales", align_bytes=64)
        nc.vector.memset(store_scales[:].bitcast(I32), 0)
        unit_row = keep.tile([P, H], F32, name="unit_row")
        nc.vector.memset(unit_row[:], 0.0)

        w_rows = w1.rearrange("(p j) c -> p j c", j=PACK)
        w_raw = []
        for h in range(2):
            raw = keep.tile([P, PACK, H // 2], F32, name="w_raw%d" % h)
            nc.sync.dma_start(out=raw[:], in_=w_rows[:, :, h * H // 2 : (h + 1) * H // 2])
            w_raw.append(raw)
            if h == 0:
                for r in range(4):
                    nc.sync.dma_start(
                        out=store_scales[r:P:32, :].bitcast(I32),
                        in_=x_scales[0, r:16:4, :].bitcast(I32),
                    )
        nc.sync.dma_start(out=unit_row[0:1, :], in_=unit.rearrange("h o -> o h"))
        store_words = keep.tile([P, T], I32, name="store_words", align_bytes=64)
        nc.sync.dma_start(
            out=store_words[:],
            in_=x_words[0].rearrange("p n r -> p (n r)").bitcast(I32),
        )
        inv_sb = keep.tile([P, PACK], F32, name="inv_sb")
        nc.sync.dma_start(out=inv_sb[:], in_=inv.rearrange("(p j) o -> p (j o)", j=PACK))
        sim_sb = keep.tile([P, S // P, V], F32, name="sim_sb")
        wt_sb = keep.tile([P, S // P, V], F32, name="wt_sb")
        nc.sync.dma_start(out=sim_sb[:], in_=sim.rearrange("(i p) v -> p i v", p=P))
        nc.sync.dma_start(out=wt_sb[:], in_=wt.rearrange("(i p) v -> p i v", p=P))

        xb_scales = keep.tile([P, V], U8, name="xb_scales", align_bytes=64)
        xa_scales = keep.tile([P, S], U8, name="xa_scales", align_bytes=64)
        nc.vector.tensor_copy(xb_scales[:], store_scales[:].indirect(list_b[:]))
        nc.vector.tensor_copy(xa_scales[:], store_scales[:].indirect(list_a[:]))

        one_half = keep.tile([P, 1], F32, name="one_half")
        nc.scalar.activation(out=one_half[:], in_=zero[:], func=ACT.Sigmoid)
        identity = keep.tile([P, P], F32, name="identity")
        make_identity(nc, identity[:])

        unit_ps = psum.tile([P, PACK, P], F32, name="unit_ps", tag="bank7")
        for t in range(PACK):
            nc.tensor.transpose(unit_ps[:, t, :], unit_row[:, t:H:PACK], identity[:])

        w_grouped = keep.tile([P, H * PACK], BF16, name="w_grouped", align_bytes=64)
        w_dst = w_grouped[:].rearrange("p (t m j) -> p m j t", t=PACK, j=PACK)
        for h in range(2):
            nc.scalar.activation(
                out=w_dst[:, h * P // 2 : (h + 1) * P // 2],
                in_=w_raw[h][:].rearrange("p j (m t) -> p m j t", t=PACK),
                func=ACT.Copy,
            )
        w_codes = keep.tile([P, H], U32, name="w_codes", align_bytes=64)
        w_scales = keep.tile([P, H], U8, name="w_scales", align_bytes=64)
        nc.vector.quantize_mx(out=w_codes[:].bitcast(FP8X4), scales=w_scales[:], in_=w_grouped[:])

        def gather_words(name, offsets, g, step):
            picked = keep.tile([P, PAIR], U32, name="%s%d" % (name, g), align_bytes=64)
            for n in range(0, PAIR, step):
                cols = slice((g * PAIR + n) // LANES, (g * PAIR + n + step) // LANES)
                nc.vector.tensor_copy(picked[:, n : n + step], store_words[:].bitcast(U32).indirect(offsets[:, cols]))
            return picked

        xb_words, xa_words = [], []
        for g in range(S // PAIR):
            xb_words.append(gather_words("xb_words", list_b, g, PAIR if g else CHUNK))
            xa_words.append(gather_words("xa_words", list_a, g, PAIR))

        first_products = []

        def steep_tanh(side, c):
            words, scales = (xa_words, xa_scales) if side == "a" else (xb_words, xb_scales)
            n0 = c * CHUNK % PAIR
            pre = psum.tile([P, PACK, CHUNK], F32, name="pre", tag="bank%d" % (len(first_products) % 4))
            first_products.append(pre)
            for t in range(PACK):
                cols = slice(t * P, (t + 1) * P)
                nc.tensor.matmul_mx(
                    out=pre[:, t, :],
                    lhsT=w_codes[:, cols].bitcast(FP8X4),
                    lhsT_scale=w_scales[:, cols],
                    rhs=words[c * CHUNK // PAIR][:, n0 : n0 + CHUNK].bitcast(FP8X4),
                    rhs_scale=scales[:, c * CHUNK : (c + 1) * CHUNK],
                    start=True,
                    stop=True,
                )
            steep = keep.tile([P, CHUNK, PACK], F32, name="steep", tag="steep_%s%d" % (side, c), align_bytes=64)
            nc.scalar.activation(
                out=steep[:], in_=pre[:].rearrange("p t n -> p n t"), func=ACT.Tanh, scale=2.0
            )
            return steep

        def chunks(rounded, c0, c1):
            return rounded[:, c0 * CHUNK * PACK : c1 * CHUNK * PACK]

        def hidden_b(c, dst, engine):
            engine.tensor_tensor(
                out=dst.rearrange("p (n t) -> p n t", t=PACK),
                in0=steep_tanh("b", c)[:],
                in1=inv_sb[:].unsqueeze(1).to_broadcast([P, CHUNK, PACK]),
                op=ALU.mult,
            )

        def hidden_a(c):
            nc.vector.scalar_tensor_tensor(
                out=chunks(ha_rounded, c, c + 1).rearrange("p (n t) -> p n t", t=PACK),
                in0=steep_tanh("a", c)[:],
                scalar=2.0 / KNEE,
                in1=unit_ps[:, :, 0].unsqueeze(1).to_broadcast([P, CHUNK, PACK]),
                op0=ALU.mult,
                op1=ALU.mult,
            )

        def quantise(codes, scales, rounded):
            nc.vector.quantize_mx(out=codes.bitcast(FP8X4), scales=scales, in_=rounded)

        hb_rounded = keep.tile([P, V * PACK], BF16, name="hb_rounded", align_bytes=64)
        hb_early = keep.tile([P, PAIR], U32, name="hb_early", align_bytes=64)
        hb_scales = keep.tile([P, V], U8, name="hb_scales", align_bytes=64)
        ha_rounded = keep.tile([P, S * PACK], BF16, name="ha_rounded", align_bytes=64)
        ha_codes = keep.tile([P, S], U32, name="ha_codes", align_bytes=64)
        ha_scales = keep.tile([P, S], U8, name="ha_scales", align_bytes=64)
        hb_codes = [hb_early]
        signed = keep.tile([P, S // P, V], F32, name="signed")
        squashed = keep.tile([P, S // P, V], F32, name="squashed")

        def score(i, u, bank):
            y = psum.tile([P, PAIR], F32, name="y", tag="bank%d" % bank)
            nc.tensor.matmul_mx(
                out=y[:],
                lhsT=ha_codes[:, i * P : (i + 1) * P].bitcast(FP8X4),
                lhsT_scale=ha_scales[:, i * P : (i + 1) * P],
                rhs=hb_codes[u][:].bitcast(FP8X4),
                rhs_scale=hb_scales[:, u * PAIR : (u + 1) * PAIR],
                start=True,
                stop=True,
            )
            return i, u, y

        def sign_and_squash(i, u, y):
            cols = slice(u * PAIR, (u + 1) * PAIR)
            nc.vector.scalar_tensor_tensor(
                out=signed[:, i, cols],
                in0=sim_sb[:, i, cols],
                scalar=one_half[:],
                in1=y[:],
                op0=ALU.subtract,
                op1=ALU.mult,
            )
            nc.scalar.activation(
                out=squashed[:, i, cols], in_=signed[:, i, cols], func=ACT.Sigmoid, scale=KNEE, bias=zero[:]
            )

        hidden_b(0, chunks(hb_rounded, 0, 1), nc.vector)
        hidden_b(1, chunks(hb_rounded, 1, 2), nc.vector)
        hidden_a(0)
        quantise(hb_early[:], hb_scales[:, 0:PAIR], chunks(hb_rounded, 0, 2))
        hidden_a(1)
        quantise(ha_codes[:, 0:PAIR], ha_scales[:, 0:PAIR], chunks(ha_rounded, 0, 2))
        first_piece = score(0, 0, 4)

        hidden_b(2, chunks(hb_rounded, 2, 3), nc.vector)
        hb_last = keep.tile([P, CHUNK * PACK], BF16, name="hb_last", tag="steep_b2", align_bytes=64)
        hidden_b(3, hb_last[:], nc.gpsimd)
        hidden_a(2)
        hidden_a(3)
        sign_and_squash(*first_piece)

        pieces = [score(1, 0, 7)]
        hb_late = keep.tile([P, PAIR], U32, name="hb_late", tag="steep_b3", align_bytes=64)
        hb_codes.append(hb_late)
        quantise(hb_late[:, CHUNK:], hb_scales[:, 3 * CHUNK :], hb_last[:])
        quantise(hb_late[:, 0:CHUNK], hb_scales[:, PAIR : 3 * CHUNK], chunks(hb_rounded, 2, 3))
        pieces.extend(score(i, 1, 5 + i) for i in range(2))
        quantise(ha_codes[:, PAIR:], ha_scales[:, PAIR:], chunks(ha_rounded, 2, 4))
        pieces.extend(score(i, u, 2 * (i - 2) + u) for i in range(2, 4) for u in range(2))
        for piece in pieces:
            sign_and_squash(*piece)

        stretch = keep.tile([P, S // P, V], F32, name="stretch")
        for i in range(S // P):
            nc.vector.scalar_tensor_tensor(
                out=stretch[:, i, :], in0=signed[:, i, :], scalar=-1.0, in1=wt_sb[:, i, :], op0=ALU.min, op1=ALU.mult
            )

        logs = keep.tile([P, S // P, V], F32, name="logs", tag="logs")
        results = keep.tile([P, S // P, V], F32, name="results")
        last = S // P - 1
        for i in range(S // P):
            rows = slice(i * P, (i + 1) * P)
            for c0 in range(0, V, PAIR):
                cols = slice(c0, c0 + PAIR)
                nc.scalar.activation(out=logs[:, i, cols], in_=squashed[:, i, cols], func=ACT.Ln, bias=TINY)
                nc.vector.scalar_tensor_tensor(
                    out=results[:, i, cols],
                    in0=logs[:, i, cols],
                    scalar=-KNEE,
                    in1=stretch[:, i, cols],
                    op0=ALU.max,
                    op1=ALU.mult,
                )
                if i == last:
                    nc.sync.dma_start(out=out[rows, cols], in_=results[:, i, cols])
            if i < last:
                nc.sync.dma_start(out=out[rows, :], in_=results[:, i, :])
